import numpy as np
import ml_dtypes


def mxq(x, axis, fmt="e4m3"):
    dtype, down = {"e4m3": (ml_dtypes.float8_e4m3fn, 7), "e5m2": (ml_dtypes.float8_e5m2, 14)}[fmt]
    v = np.moveaxis(np.asarray(x, np.float32).astype(ml_dtypes.bfloat16).astype(np.float64), axis, -1)
    blocks = v.reshape(v.shape[:-1] + (-1, 32))
    amax = np.abs(blocks).max(-1, keepdims=True)
    byte = np.maximum(np.where(amax > 0, np.frexp(amax)[1] - 1 + 127, 0) - down, 1)
    scale = np.exp2(byte - 127.0)
    codes = (blocks / scale).astype(np.float32).astype(dtype).astype(np.float64)
    return np.moveaxis((codes * scale).reshape(v.shape), -1, axis)


WIDE = False


def mx_kscale(k):
    if not WIDE:
        return np.ones(k)
    levels = np.array([10, -10, 5, -5, 0])
    if k % 512:
        return np.exp2(np.random.permutation(np.resize(levels, k // 32))).repeat(32)
    a = np.empty((k // 512, 16))
    for p in range(k // 512):
        a[p, :8] = np.random.permutation(np.resize(levels, 8))
        for g in range(8):
            far = levels[np.abs(levels - a[p, g]) >= 10]
            a[p, g + 8] = far[np.random.randint(len(far))]
    return np.exp2(a.ravel()).repeat(32)


def f64(x):
    return np.asarray(x).astype(np.float64)


def striped(idx):
    return np.tile(np.asarray(idx).reshape(-1, 16).T, (8, 1)).astype(np.uint16)


def unstriped(offs):
    return offs[:16].T.reshape(-1).astype(np.int64)


E2M1 = np.array([0.0, 0.5, 1.0, 1.5, 2.0, 3.0, 4.0, 6.0, -0.0, -0.5, -1.0, -1.5, -2.0, -3.0, -4.0, -6.0])


def pack_weight(w, fmt):
    k, n = w.shape
    w = f64(np.asarray(w, np.float32).astype(ml_dtypes.bfloat16)).reshape(k // 32, 32, n)
    amax = np.abs(w).max(1)
    if fmt == "e4m3":
        byte = np.frexp(amax)[1] - 1 + 127 - 7
    else:
        mant, ex = np.frexp(amax / 6.0)
        byte = np.where(mant > 0.5, ex, ex - 1) + 127
    byte = np.clip(np.where(amax > 0, byte, 1), 1, 254)
    scaled = (w * np.exp2(127.0 - byte)[:, None, :]).reshape(k, n).astype(np.float32)
    by_word = np.ascontiguousarray(scaled.reshape(k // 512, 128, 4, n).transpose(0, 1, 3, 2))
    if fmt == "e4m3":
        words = by_word.astype(ml_dtypes.float8_e4m3fn).view(np.uint8)
    else:
        c = by_word.astype(ml_dtypes.float4_e2m1fn).view(np.uint8) & 0xF
        words = (c[..., 0::2] | (c[..., 1::2] << 4)).reshape(k // 512, 128, 2 * n)
    return np.ascontiguousarray(words), np.ascontiguousarray(byte.astype(np.uint8).reshape(k // 512, 16, n))


def unpack_weight(words, scales, fmt):
    g, _, n = scales.shape
    words = np.ascontiguousarray(words).reshape(g, 128, n, -1)
    if fmt == "e4m3":
        vals = words.view(ml_dtypes.float8_e4m3fn).astype(np.float64)
    else:
        nib = np.empty((g, 128, n, 4), np.uint8)
        nib[..., 0::2] = words & 0xF
        nib[..., 1::2] = words >> 4
        vals = E2M1[nib]
    vals = vals * np.repeat(np.exp2(scales.astype(np.float64) - 127.0), 8, axis=1)[..., None]
    return vals.transpose(0, 1, 3, 2).reshape(g * 512, n)


def softplus(v):
    return np.log(1.0 + np.exp(v))


D, E, T, I, Q, G = 512, 512, 1024, 256, 512, 32


def setup_inputs():
    n = np.random.standard_normal
    idx = np.random.permutation(T)[:I]
    fd = mx_kscale(D)
    fq = mx_kscale(Q)
    keysp = pack_weight(n((D, T)) / fd[:, None], "e2m1")
    return {
        "query": (n((D, Q)) * 0.8 / np.sqrt(D) * fd[:, None]).astype(np.float32),
        "query2": (n((D, Q)) * 1.0 / np.sqrt(D) * fd[:, None]).astype(np.float32),
        "keys_words": keysp[0],
        "keys_scales": keysp[1],
        "reserve": (np.random.uniform(2.0, 10.0, (Q, 1))).astype(np.float32),
        "qs": (np.random.uniform(2.0, 8.0, (Q, 1)) * fq[:, None]).astype(np.float32),
        "grows": (n((Q, E)) / fq[:, None]).astype(np.float32),
        "old": (n((E, T)) * 2.0).astype(np.float32),
        "fade": (np.random.uniform(0.5, 1.0, (1, T))).astype(np.float32),
        "offs": striped(idx),
    }


def reference(query, query2, keys_words, keys_scales, reserve, qs, grows, old, fade, offs):
    idx = unstriped(offs)
    keysu = unpack_weight(keys_words, keys_scales, "e2m1")
    queryq = mxq(f64(query), 0, "e4m3")
    keysidxg = keysu[:, idx]
    a = queryq.T @ keysidxg
    query2q = mxq(f64(query2), 0, "e4m3")
    b = query2q.T @ keysidxg
    m1 = b.reshape(Q, G, I // G).mean(axis=2)
    q0 = softplus(m1 * 3.0)
    z = np.sum(q0, axis=1, keepdims=True) + f64(reserve)
    pa = np.exp(a)
    s = pa.reshape(Q, G, I // G).sum(axis=2)
    r = q0 / s / z
    rr = np.repeat(r, I // G, axis=1)
    w = pa * rr
    wq = w * f64(qs)
    growsq = mxq(f64(grows), 0, "e4m3")
    wqq = mxq(wq, 0, "e4m3")
    gv = growsq.T @ wqq
    gf = np.zeros((E, T))
    gf[:, idx] = gv
    y = f64(old) * f64(fade) + gf
    return y

@@ -1,0 +1,321 @@
+from contextlib import ExitStack
+
+import concourse.mybir as mybir
+from concourse.masks import make_identity
+
+D, E, T, I, Q = 512, 512, 1024, 256, 512
+FLOPS = 2 * (2 * D * Q * I + Q * E * I)
+
+F32 = mybir.dt.float32
+BF16 = mybir.dt.bfloat16
+I32 = mybir.dt.int32
+U32 = mybir.dt.uint32
+U16 = mybir.dt.uint16
+U8 = mybir.dt.uint8
+FP8X4 = mybir.dt.float8_e4m3fn_x4
+FP4X4 = mybir.dt.float4_e2m1fn_x4
+ALU = mybir.AluOpType
+ACT = mybir.ActivationFunctionType
+AX = mybir.AxisListType
+
+P = 128
+PACK = 4
+PAGE = 8
+G = I // PAGE
+HALF = I // 2
+GH = G // 2
+BANK = 512
+ROW = 40
+ROUTE = ["V","V","V","V"]
+
+
+def tile_attend_bpagequotas_v_kernel(tc, query, query2, keys_words, keys_scales, reserve, qs, grows, old, fade, offs, out):
+    nc = tc.nc
+    with ExitStack() as ctx:
+        sb = ctx.enter_context(tc.tile_pool(name="sb", bufs=1))
+        ps = ctx.enter_context(tc.psum_pool(name="ps", bufs=1))
+
+        def bank(tag, name):
+            return ps.tile([P, PACK, P], F32, name=name, tag=tag)
+
+        offsets = sb.tile([P, I // 16], U16, name="offsets")
+        nc.sync.dma_start(offsets[:], offs)
+        key_words = sb.tile([P, T], U16, name="key_words", align_bytes=64)
+        nc.sync.dma_start(out=key_words[:].bitcast(I32), in_=keys_words[0].bitcast(I32))
+        key_scales = sb.tile([P, T], U8, name="key_scales", align_bytes=64)
+        nc.vector.memset(key_scales[:].bitcast(I32), 0)
+        for quad in range(4):
+            nc.sync.dma_start(
+                out=key_scales[32 * quad : 32 * quad + 4, :].bitcast(I32),
+                in_=keys_scales[0, 4 * quad : 4 * quad + 4, :].bitcast(I32),
+            )
+
+        def load_query(src, name):
+            rows = src.rearrange("(p j) q -> p j q", j=PACK)
+            parts = []
+            for h in range(2):
+                raw = sb.tile([P, PACK, Q // 2], F32, name=f"{name}_raw{h}")
+                nc.sync.dma_start(out=raw[:], in_=rows[:, :, h * (Q // 2) : (h + 1) * (Q // 2)])
+                parts.append(raw)
+            return parts
+
+        q1_raw = load_query(query, "q1")
+        q2_raw = load_query(query2, "q2")
+        qs_sb = sb.tile([P, PACK], F32, name="qs_sb")
+        nc.sync.dma_start(out=qs_sb[:], in_=qs.rearrange("(p t) o -> p (t o)", t=PACK))
+        reserve_sb = sb.tile([P, PACK], F32, name="reserve_sb")
+        nc.sync.dma_start(out=reserve_sb[:], in_=reserve.rearrange("(p t) o -> p (t o)", t=PACK))
+        grows_raw = sb.tile([P, PACK, E], F32, name="grows_raw")
+        nc.sync.dma_start(out=grows_raw[:], in_=grows.rearrange("(p j) e -> p j e", j=PACK))
+        fade_rows = sb.tile([P, P], F32, name="fade_rows")
+        nc.vector.memset(fade_rows[:], 0.0)
+        nc.sync.dma_start(out=fade_rows[0 : T // P, :], in_=fade.rearrange("o (c n) -> (o c) n", n=P))
+        old_sb = []
+        for k in range(E // P):
+            old_k = sb.tile([P, T], F32, name=f"old{k}")
+            nc.sync.dma_start(out=old_k[:], in_=old[k * P : (k + 1) * P, :])
+            old_sb.append(old_k)
+
+        ident = sb.tile([P, P], F32, name="ident")
+        make_identity(nc, ident[:])
+        placed = []
+        for k in range(2):
+            placed_k = sb.tile([P, T], F32, name=f"placed{k}")
+            nc.vector.memset(placed_k[:], 0.0)
+            placed.append(placed_k)
+
+        kg = sb.tile([P, I], U16, name="kg", align_bytes=64)
+        nc.vector.tensor_copy(kg[:], key_words[:].indirect(offsets[:]))
+        sg = sb.tile([P, I], U8, name="sg", align_bytes=64)
+        nc.vector.tensor_copy(sg[:], key_scales[:].indirect(offsets[:]))
+
+        def interleave_query(raw, grouped, h, n):
+            src = raw[:].rearrange("p j (s t) -> p s j t", t=PACK)
+            dst = grouped[:, :, 64 * h : 64 * (h + 1), :].rearrange("p t s j -> p s j t")
+            nc.scalar.copy(out=dst[:, 0:n], in_=src[:, 0:n])
+            nc.vector.tensor_copy(out=dst[:, n:64], in_=src[:, n:64])
+
+        def quantize_query(grouped, codes, scales, lo, hi):
+            for t in range(PACK):
+                cols = slice(t * P + lo, t * P + hi)
+                nc.vector.quantize_mx(
+                    out=codes[:, cols].bitcast(FP8X4), scales=scales[:, cols], in_=grouped[:, t, lo:hi, :].rearrange("p s j -> p (s j)")
+                )
+
+        q1_grouped = sb.tile([P, PACK, P, PACK], BF16, name="q1_grouped", align_bytes=64)
+        q1_codes = sb.tile([P, Q], U32, name="q1_codes", align_bytes=64)
+        q1_scales = sb.tile([P, Q], U8, name="q1_scales", align_bytes=64)
+        interleave_query(q1_raw[0], q1_grouped, 0, 24)
+        interleave_query(q1_raw[1], q1_grouped, 1, 20)
+        quantize_query(q1_grouped, q1_codes, q1_scales, 0, P)
+        pa = sb.tile([P, PAGE, G, PACK], F32, name="pa", tag="wide")
+        for h in range(2):
+            a_ps = bank(f"r{2 + h}", f"a_ps{h}")
+            slots = slice(h * HALF, (h + 1) * HALF)
+            for t in range(PACK):
+                cols = slice(t * P, (t + 1) * P)
+                nc.tensor.matmul_mx(
+                    out=a_ps[:, t, :],
+                    lhsT=q1_codes[:, cols].bitcast(FP8X4),
+                    lhsT_scale=q1_scales[:, cols],
+                    rhs=kg[:, slots].bitcast(FP4X4),
+                    rhs_scale=sg[:, slots],
+                    start=True,
+                    stop=True,
+                )
+            nc.scalar.activation(
+                out=pa[:, :, h * GH : (h + 1) * GH, :], in_=a_ps[:].rearrange("p t (g j) -> p j g t", j=PAGE), func=ACT.Exp
+            )
+
+        q2_grouped = sb.tile([P, PACK, P, PACK], BF16, name="q2_grouped", align_bytes=64)
+        q2_codes = sb.tile([P, Q], U32, name="q2_codes", align_bytes=64)
+        q2_scales = sb.tile([P, Q], U8, name="q2_scales", align_bytes=64)
+        interleave_query(q2_raw[1], q2_grouped, 1, 20)
+        quantize_query(q2_grouped, q2_codes, q2_scales, 64, P)
+        interleave_query(q2_raw[0], q2_grouped, 0, 32)
+        quantize_query(q2_grouped, q2_codes, q2_scales, 0, 64)
+        kb = sb.tile([P, I], U16, name="kb", align_bytes=64)
+        nc.vector.tensor_copy(
+            out=kb[:].rearrange("p (u g j) -> p g u j", u=2, j=4), in_=kg[:].rearrange("p (g u j) -> p g u j", u=2, j=4)
+        )
+        sbb = sb.tile([P, I], U8, name="sbb", align_bytes=64)
+        nc.vector.tensor_copy(
+            out=sbb[:].rearrange("p (u g j) -> p g u j", u=2, j=4), in_=sg[:].rearrange("p (g u j) -> p g u j", u=2, j=4)
+        )
+        b_ps = bank("g1", "b_ps")
+        for t in range(PACK):
+            cols = slice(t * P, (t + 1) * P)
+            for u in range(2):
+                slots = slice(u * HALF, (u + 1) * HALF)
+                nc.tensor.matmul_mx(
+                    out=b_ps[:, t, :],
+                    lhsT=q2_codes[:, cols].bitcast(FP8X4),
+                    lhsT_scale=q2_scales[:, cols],
+                    rhs=kb[:, slots].bitcast(FP4X4),
+                    rhs_scale=sbb[:, slots],
+                    start=(u == 0),
+                    stop=(u == 1),
+                )
+        msum = sb.tile([P, PACK, G], F32, name="msum")
+        nc.vector.tensor_reduce(out=msum[:], in_=b_ps[:].rearrange("p t (g j) -> p t g j", j=4), axis=AX.X, op=ALU.add)
+        mabs = sb.tile([P, PACK, G], F32, name="mabs")
+        nc.scalar.activation(out=mabs[:], in_=msum[:], func=ACT.Abs, scale=3.0 / PAGE)
+        mexp = sb.tile([P, PACK, G], F32, name="mexp")
+        nc.scalar.activation(out=mexp[:], in_=mabs[:], func=ACT.Exp, scale=-1.0)
+        soft = sb.tile([P, PACK, ROW], F32, name="soft")
+        nc.scalar.activation(out=soft[:, :, 0:G], in_=mexp[:], func=ACT.Ln, bias=1.0)
+
+        relu = sb.tile([P, PACK, ROW], F32, name="relu")
+        nc.vector.tensor_copy(out=relu[:, :, G], in_=reserve_sb[:])
+        nc.vector.tensor_scalar(out=relu[:, :, 0:G], in0=msum[:], scalar1=3.0 / PAGE, scalar2=0.0, op0=ALU.mult, op1=ALU.max)
+        nc.vector.tensor_reduce(out=soft[:, :, G], in_=relu[:, :, 0 : G + 1], axis=AX.X, op=ALU.add)
+        z = sb.tile([P, PACK], F32, name="z")
+        nc.vector.tensor_reduce(out=z[:], in_=soft[:, :, 0 : G + 1], axis=AX.X, op=ALU.add)
+        quota = sb.tile([P, G, PACK], F32, name="quota")
+        nc.vector.tensor_tensor(
+            out=quota[:], in0=soft[:, :, 0:G].rearrange("p t g -> p g t"), in1=relu[:, :, 0:G].rearrange("p t g -> p g t"), op=ALU.add
+        )
+        inv_z = sb.tile([P, PACK], F32, name="inv_z")
+        nc.vector.reciprocal(out=inv_z[:], in_=z[:])
+
+        sum_ps = bank("f0", "sum_ps")
+        for j in range(PAGE):
+            nc.tensor.matmul(
+                sum_ps[:, 0, :], pa[:, j].rearrange("p g t -> p (g t)"), ident[:], is_transpose=True, start=(j == 0), stop=(j == PAGE - 1)
+            )
+        inv_turned = sb.tile([P, P], F32, name="inv_turned")
+        for n in range(4):
+            nc.vector.reciprocal(out=inv_turned[:, 32 * n : 32 * (n + 1)], in_=sum_ps[:, 0, 32 * n : 32 * (n + 1)])
+        inv_ps = bank("f1", "inv_ps")
+        nc.tensor.transpose(inv_ps[:, 0, :], inv_turned[:], ident[:])
+        share = sb.tile([P, G, PACK], F32, name="share")
+        nc.vector.tensor_tensor(
+            out=share[:],
+            in0=inv_ps[:, 0, :].rearrange("p (g t) -> p g t", t=PACK),
+            in1=qs_sb[:].unsqueeze(1).broadcast_to([P, G, PACK]),
+            op=ALU.mult,
+        )
+        unnormed = sb.tile([P, G, PACK], F32, name="unnormed")
+        nc.vector.tensor_tensor(out=unnormed[:], in0=quota[:], in1=share[:], op=ALU.mult)
+        factor = sb.tile([P, G, PACK], F32, name="factor")
+        nc.vector.tensor_tensor(out=factor[:], in0=unnormed[:], in1=inv_z[:].unsqueeze(1).broadcast_to([P, G, PACK]), op=ALU.mult)
+
+        w_codes = sb.tile([P, I], U32, name="w_codes", align_bytes=64)
+        w_scales = sb.tile([P, I], U8, name="w_scales", align_bytes=64)
+        for h in range(2):
+            wq = sb.tile([P, HALF, PACK], BF16, name=f"wq{h}", align_bytes=64)
+            nc.vector.tensor_tensor(
+                out=wq[:].rearrange("p (g j) t -> p g j t", j=PAGE),
+                in0=pa[:, :, h * GH : (h + 1) * GH, :].rearrange("p j g t -> p g j t"),
+                in1=factor[:, h * GH : (h + 1) * GH, :].unsqueeze(2).broadcast_to([P, GH, PAGE, PACK]),
+                op=ALU.mult,
+            )
+            slots = slice(h * HALF, (h + 1) * HALF)
+            nc.vector.quantize_mx(out=w_codes[:, slots].bitcast(FP8X4), scales=w_scales[:, slots], in_=wq[:].rearrange("p i t -> p (i t)"))
+
+        grows_grouped = sb.tile([P, E, PACK], BF16, name="grows_grouped", align_bytes=64)
+        src = grows_raw[:].rearrange("p j (c i) -> p c j i", i=4)
+        dst = grows_grouped[:].rearrange("p (c i) j -> p c j i", i=4)
+        g_codes = sb.tile([P, E], U32, name="g_codes", align_bytes=64)
+        g_scales = sb.tile([P, E], U8, name="g_scales", align_bytes=64)
+        for k in range(E // P):
+            if k < 3:
+                nc.vector.tensor_copy(out=dst[:, 32 * k : 32 * (k + 1)], in_=src[:, 32 * k : 32 * (k + 1)])
+            else:
+                nc.scalar.copy(out=dst[:, 32 * k : 32 * (k + 1)], in_=src[:, 32 * k : 32 * (k + 1)])
+            cols = slice(k * P, (k + 1) * P)
+            nc.vector.quantize_mx(
+                out=g_codes[:, cols].bitcast(FP8X4), scales=g_scales[:, cols], in_=grows_grouped[:, cols, :].rearrange("p e j -> p (e j)")
+            )
+
+        pieces = [(0, 0, HALF), (0, HALF, I)] + [(k, 0, I) for k in range(1, E // P)]
+        gv = [sb.tile([P, I], F32, name=f"gv{k}") for k in range(E // P)]
+        for n, (k, lo, hi) in enumerate(pieces):
+            gv_ps = ps.tile([P, BANK], F32, name=f"gv_ps{n}", tag=f"g{(n + 1) % 2}")
+            cols = slice(k * P, (k + 1) * P)
+            nc.tensor.matmul_mx(
+                out=gv_ps[:, 0 : hi - lo],
+                lhsT=g_codes[:, cols].bitcast(FP8X4),
+                lhsT_scale=g_scales[:, cols],
+                rhs=w_codes[:, lo:hi].bitcast(FP8X4),
+                rhs_scale=w_scales[:, lo:hi],
+                start=True,
+                stop=True,
+            )
+            nc.scalar.copy(out=gv[k][:, lo:hi], in_=gv_ps[:, 0 : hi - lo])
+
+        fade_ps = bank("r0", "fade_ps")
+        nc.tensor.transpose(fade_ps[:, 0, :], fade_rows[:], ident[:])
+        fade_cols = sb.tile([P, T // P], F32, name="fade_cols")
+        nc.scalar.copy(out=fade_cols[:], in_=fade_ps[:, 0, 0 : T // P])
+
+        fade_wide = None
+
+        def turn_and_fade(k):
+            turned = sb.tile([P, T // P, P], F32, name=f"turned{k}", tag="turned", bufs=2)
+            for u in range(2):
+                fwd = bank(f"f{u}", f"fwd{k}_{u}")
+                for c in range(4):
+                    blk = 4 * u + c
+                    nc.tensor.transpose(fwd[:, c, :], old_sb[k][:, blk * P : (blk + 1) * P], ident[:])
+                for c in range(4):
+                    blk = 4 * u + c
+                    nc.scalar.activation(out=turned[:, blk, :], in_=fwd[:, c, :], func=ACT.Copy, scale=fade_cols[:, blk : blk + 1])
+            return turned
+
+        def turn_back(k, turned):
+            back = []
+            for u in range(2):
+                bk = bank(f"r{2 * (k % 2) + u}", f"back{k}_{u}")
+                for c in range(4):
+                    nc.tensor.transpose(bk[:, c, :], turned[:, 4 * u + c, :], ident[:])
+                back.append(bk)
+            return back
+
+        def store(k, u, res):
+            nc.sync.dma_start(out=out[k * P : (k + 1) * P, u * BANK : (u + 1) * BANK], in_=res)
+
+        for k in range(E // P):
+            route = ROUTE[k]
+            window = placed[k % len(placed)]
+            if route == "GG":
+                faded = sb.tile([P, T], F32, name=f"faded{k}", tag="wide")
+                nc.gpsimd.tensor_tensor(out=faded[:], in0=old_sb[k][:], in1=fade_wide[:], op=ALU.mult)
+            else:
+                turned = turn_and_fade(k)
+            if route in ("V", "G"):
+                back = turn_back(k, turned)
+            if route == "G":
+                faded = sb.tile([P, T], F32, name=f"faded{k}")
+                for u in range(2):
+                    nc.scalar.copy(out=faded[:, u * BANK : (u + 1) * BANK], in_=back[u][:].rearrange("p c n -> p (c n)"))
+            for kk, lo, hi in pieces:
+                if kk == k:
+                    nc.vector.tensor_copy(window[:].indirect(offsets[:, lo // 16 : hi // 16]), gv[k][:, lo:hi])
+            if route in ("G", "GG"):
+                res = sb.tile([P, T], F32, name=f"res{k}")
+                nc.gpsimd.tensor_tensor(out=res[:], in0=faded[:], in1=window[:], op=ALU.add)
+                nc.sync.dma_start(out=out[k * P : (k + 1) * P, :], in_=res[:])
+            if route == "V":
+                for u in range(2):
+                    res = sb.tile([P, BANK], F32, name=f"res{k}_{u}")
+                    cols = slice(u * BANK, (u + 1) * BANK)
+                    nc.vector.tensor_tensor(out=res[:], in0=back[u][:].rearrange("p c n -> p (c n)"), in1=window[:, cols], op=ALU.add)
+                    store(k, u, res[:])
+            if route == "S":
+                placed_turned = sb.tile([P, T // P, P], F32, name=f"placed_turned{k}", tag="placed_turned")
+                for u in range(2):
+                    fwd = bank(f"f{u}", f"pfwd{k}_{u}")
+                    for c in range(4):
+                        blk = 4 * u + c
+                        nc.tensor.transpose(fwd[:, c, :], window[:, blk * P : (blk + 1) * P], ident[:])
+                    nc.scalar.copy(out=placed_turned[:, 4 * u : 4 * u + 4, :], in_=fwd[:])
+                for u in range(2):
+                    bk = bank(f"r{2 * (k % 2) + u}", f"sum{k}_{u}")
+                    for c in range(4):
+                        blk = 4 * u + c
+                        nc.tensor.matmul(bk[:, c, :], turned[:, blk, :], ident[:], is_transpose=True, start=True, stop=False)
+                        nc.tensor.matmul(bk[:, c, :], placed_turned[:, blk, :], ident[:], is_transpose=True, start=False, stop=True)
+                    res = sb.tile([P, BANK], F32, name=f"res{k}_{u}")
+                    nc.scalar.copy(out=res[:], in_=bk[:].rearrange("p c n -> p (c n)"))
+                    store(k, u, res[:])

@@ -26,7 +26,8 @@ HALF = I // 2
 GH = G // 2
 BANK = 512
 ROW = 40
-ROUTE = ["V","V","V","V"]
+BACK = [["r0","r1"],["r2","r3"],["r0","r1"],["r2","r3"]]
+ROUTE = ["G","G","V","V"]
 
 
 def tile_attend_bpagequotas_v_kernel(tc, query, query2, keys_words, keys_scales, reserve, qs, grows, old, fade, offs, out):
@@ -79,9 +80,9 @@ def tile_attend_bpagequotas_v_kernel(tc, query, query2, keys_words, keys_scales,
         ident = sb.tile([P, P], F32, name="ident")
         make_identity(nc, ident[:])
         placed = []
-        for k in range(2):
+        for k in range(4):
             placed_k = sb.tile([P, T], F32, name=f"placed{k}")
-            nc.vector.memset(placed_k[:], 0.0)
+            (nc.vector if k < 2 else nc.gpsimd).memset(placed_k[:], 0.0)
             placed.append(placed_k)
 
         kg = sb.tile([P, I], U16, name="kg", align_bytes=64)
@@ -89,11 +90,22 @@ def tile_attend_bpagequotas_v_kernel(tc, query, query2, keys_words, keys_scales,
         sg = sb.tile([P, I], U8, name="sg", align_bytes=64)
         nc.vector.tensor_copy(sg[:], key_scales[:].indirect(offsets[:]))
 
+        kb = sb.tile([P, I], U16, name="kb", align_bytes=64)
+        nc.vector.tensor_copy(
+            out=kb[:].rearrange("p (u g j) -> p g u j", u=2, j=4), in_=kg[:].rearrange("p (g u j) -> p g u j", u=2, j=4)
+        )
+        sbb = sb.tile([P, I], U8, name="sbb", align_bytes=64)
+        nc.vector.tensor_copy(
+            out=sbb[:].rearrange("p (u g j) -> p g u j", u=2, j=4), in_=sg[:].rearrange("p (g u j) -> p g u j", u=2, j=4)
+        )
+
         def interleave_query(raw, grouped, h, n):
             src = raw[:].rearrange("p j (s t) -> p s j t", t=PACK)
             dst = grouped[:, :, 64 * h : 64 * (h + 1), :].rearrange("p t s j -> p s j t")
-            nc.scalar.copy(out=dst[:, 0:n], in_=src[:, 0:n])
-            nc.vector.tensor_copy(out=dst[:, n:64], in_=src[:, n:64])
+            if n > 0:
+                nc.scalar.copy(out=dst[:, 0:n], in_=src[:, 0:n])
+            if n < 64:
+                nc.vector.tensor_copy(out=dst[:, n:64], in_=src[:, n:64])
 
         def quantize_query(grouped, codes, scales, lo, hi):
             for t in range(PACK):
@@ -105,8 +117,8 @@ def tile_attend_bpagequotas_v_kernel(tc, query, query2, keys_words, keys_scales,
         q1_grouped = sb.tile([P, PACK, P, PACK], BF16, name="q1_grouped", align_bytes=64)
         q1_codes = sb.tile([P, Q], U32, name="q1_codes", align_bytes=64)
         q1_scales = sb.tile([P, Q], U8, name="q1_scales", align_bytes=64)
-        interleave_query(q1_raw[0], q1_grouped, 0, 24)
-        interleave_query(q1_raw[1], q1_grouped, 1, 20)
+        interleave_query(q1_raw[0], q1_grouped, 0, 64)
+        interleave_query(q1_raw[1], q1_grouped, 1, 24)
         quantize_query(q1_grouped, q1_codes, q1_scales, 0, P)
         pa = sb.tile([P, PAGE, G, PACK], F32, name="pa", tag="wide")
         for h in range(2):
@@ -118,30 +130,21 @@ def tile_attend_bpagequotas_v_kernel(tc, query, query2, keys_words, keys_scales,
                     out=a_ps[:, t, :],
                     lhsT=q1_codes[:, cols].bitcast(FP8X4),
                     lhsT_scale=q1_scales[:, cols],
-                    rhs=kg[:, slots].bitcast(FP4X4),
-                    rhs_scale=sg[:, slots],
+                    rhs=kb[:, slots].bitcast(FP4X4),
+                    rhs_scale=sbb[:, slots],
                     start=True,
                     stop=True,
                 )
             nc.scalar.activation(
-                out=pa[:, :, h * GH : (h + 1) * GH, :], in_=a_ps[:].rearrange("p t (g j) -> p j g t", j=PAGE), func=ACT.Exp
+                out=pa[:, 4 * h : 4 * (h + 1)], in_=a_ps[:].rearrange("p t (g j) -> p j g t", j=4), func=ACT.Exp
             )
 
         q2_grouped = sb.tile([P, PACK, P, PACK], BF16, name="q2_grouped", align_bytes=64)
         q2_codes = sb.tile([P, Q], U32, name="q2_codes", align_bytes=64)
         q2_scales = sb.tile([P, Q], U8, name="q2_scales", align_bytes=64)
-        interleave_query(q2_raw[1], q2_grouped, 1, 20)
-        quantize_query(q2_grouped, q2_codes, q2_scales, 64, P)
-        interleave_query(q2_raw[0], q2_grouped, 0, 32)
-        quantize_query(q2_grouped, q2_codes, q2_scales, 0, 64)
-        kb = sb.tile([P, I], U16, name="kb", align_bytes=64)
-        nc.vector.tensor_copy(
-            out=kb[:].rearrange("p (u g j) -> p g u j", u=2, j=4), in_=kg[:].rearrange("p (g u j) -> p g u j", u=2, j=4)
-        )
-        sbb = sb.tile([P, I], U8, name="sbb", align_bytes=64)
-        nc.vector.tensor_copy(
-            out=sbb[:].rearrange("p (u g j) -> p g u j", u=2, j=4), in_=sg[:].rearrange("p (g u j) -> p g u j", u=2, j=4)
-        )
+        interleave_query(q2_raw[1], q2_grouped, 1, 0)
+        interleave_query(q2_raw[0], q2_grouped, 0, 64)
+        quantize_query(q2_grouped, q2_codes, q2_scales, 0, P)
         b_ps = bank("g1", "b_ps")
         for t in range(PACK):
             cols = slice(t * P, (t + 1) * P)
@@ -252,7 +255,7 @@ def tile_attend_bpagequotas_v_kernel(tc, query, query2, keys_words, keys_scales,
         fade_wide = None
 
         def turn_and_fade(k):
-            turned = sb.tile([P, T // P, P], F32, name=f"turned{k}", tag="turned", bufs=2)
+            turned = sb.tile([P, T // P, P], F32, name=f"turned{k}")
             for u in range(2):
                 fwd = bank(f"f{u}", f"fwd{k}_{u}")
                 for c in range(4):
@@ -266,7 +269,7 @@ def tile_attend_bpagequotas_v_kernel(tc, query, query2, keys_words, keys_scales,
         def turn_back(k, turned):
             back = []
             for u in range(2):
-                bk = bank(f"r{2 * (k % 2) + u}", f"back{k}_{u}")
+                bk = bank(BACK[k][u], f"back{k}_{u}")
                 for c in range(4):
                     nc.tensor.transpose(bk[:, c, :], turned[:, 4 * u + c, :], ident[:])
                 back.append(bk)

@@ -26,8 +26,9 @@ HALF = I // 2
 GH = G // 2
 BANK = 512
 ROW = 40
-BACK = [["r0","r1"],["r2","r3"],["r0","r1"],["r2","r3"]]
-ROUTE = ["G","G","V","V"]
+BACK = [["r0","r1"],["r3","g0"],["f0","f1"],["r0","r1"]]
+FWD = [["f0","f1"],["f0","g0"],["g1","r2"],["g1","r2"]]
+TURNED = {(0, 0): "mexp"}
 
 
 def tile_attend_bpagequotas_v_kernel(tc, query, query2, keys_words, keys_scales, reserve, qs, grows, old, fade, offs, out):
@@ -50,27 +51,27 @@ def tile_attend_bpagequotas_v_kernel(tc, query, query2, keys_words, keys_scales,
                 out=key_scales[32 * quad : 32 * quad + 4, :].bitcast(I32),
                 in_=keys_scales[0, 4 * quad : 4 * quad + 4, :].bitcast(I32),
             )
+        fade_rows = sb.tile([P, P], F32, name="fade_rows")
+        nc.vector.memset(fade_rows[:], 0.0)
+        nc.sync.dma_start(out=fade_rows[0 : T // P, :], in_=fade.rearrange("o (c n) -> (o c) n", n=P))
 
         def load_query(src, name):
             rows = src.rearrange("(p j) q -> p j q", j=PACK)
             parts = []
             for h in range(2):
-                raw = sb.tile([P, PACK, Q // 2], F32, name=f"{name}_raw{h}")
+                raw = sb.tile([P, PACK, Q // 2], F32, name=f"{name}_raw{h}", tag=("wide" if (name, h) == ("q2", 1) else f"{name}_raw{h}"), align_bytes=64)
                 nc.sync.dma_start(out=raw[:], in_=rows[:, :, h * (Q // 2) : (h + 1) * (Q // 2)])
                 parts.append(raw)
             return parts
 
         q1_raw = load_query(query, "q1")
-        q2_raw = load_query(query2, "q2")
-        qs_sb = sb.tile([P, PACK], F32, name="qs_sb")
-        nc.sync.dma_start(out=qs_sb[:], in_=qs.rearrange("(p t) o -> p (t o)", t=PACK))
         reserve_sb = sb.tile([P, PACK], F32, name="reserve_sb")
         nc.sync.dma_start(out=reserve_sb[:], in_=reserve.rearrange("(p t) o -> p (t o)", t=PACK))
+        q2_raw = load_query(query2, "q2")
         grows_raw = sb.tile([P, PACK, E], F32, name="grows_raw")
         nc.sync.dma_start(out=grows_raw[:], in_=grows.rearrange("(p j) e -> p j e", j=PACK))
-        fade_rows = sb.tile([P, P], F32, name="fade_rows")
-        nc.vector.memset(fade_rows[:], 0.0)
-        nc.sync.dma_start(out=fade_rows[0 : T // P, :], in_=fade.rearrange("o (c n) -> (o c) n", n=P))
+        qs_sb = sb.tile([P, PACK], F32, name="qs_sb")
+        nc.sync.dma_start(out=qs_sb[:], in_=qs.rearrange("(p t) o -> p (t o)", t=PACK))
         old_sb = []
         for k in range(E // P):
             old_k = sb.tile([P, T], F32, name=f"old{k}")
@@ -80,9 +81,9 @@ def tile_attend_bpagequotas_v_kernel(tc, query, query2, keys_words, keys_scales,
         ident = sb.tile([P, P], F32, name="ident")
         make_identity(nc, ident[:])
         placed = []
-        for k in range(4):
+        for k in range(3):
             placed_k = sb.tile([P, T], F32, name=f"placed{k}")
-            (nc.vector if k < 2 else nc.gpsimd).memset(placed_k[:], 0.0)
+            (nc.vector if k < 3 else nc.gpsimd).memset(placed_k[:], 0.0)
             placed.append(placed_k)
 
         kg = sb.tile([P, I], U16, name="kg", align_bytes=64)
@@ -117,10 +118,15 @@ def tile_attend_bpagequotas_v_kernel(tc, query, query2, keys_words, keys_scales,
         q1_grouped = sb.tile([P, PACK, P, PACK], BF16, name="q1_grouped", align_bytes=64)
         q1_codes = sb.tile([P, Q], U32, name="q1_codes", align_bytes=64)
         q1_scales = sb.tile([P, Q], U8, name="q1_scales", align_bytes=64)
-        interleave_query(q1_raw[0], q1_grouped, 0, 64)
-        interleave_query(q1_raw[1], q1_grouped, 1, 24)
+        interleave_query(q1_raw[0], q1_grouped, 0, 48)
+        interleave_query(q1_raw[1], q1_grouped, 1, 20)
         quantize_query(q1_grouped, q1_codes, q1_scales, 0, P)
-        pa = sb.tile([P, PAGE, G, PACK], F32, name="pa", tag="wide")
+        q2_grouped = sb.tile([P, PACK, P, PACK], BF16, name="q2_grouped", align_bytes=64)
+        q2_codes = sb.tile([P, Q], U32, name="q2_codes", align_bytes=64)
+        q2_scales = sb.tile([P, Q], U8, name="q2_scales", align_bytes=64)
+        interleave_query(q2_raw[1], q2_grouped, 1, 20)
+        interleave_query(q2_raw[0], q2_grouped, 0, 40)
+        pa = sb.tile([P, PAGE, G, PACK], F32, name="pa", tag="wide", align_bytes=64)
         for h in range(2):
             a_ps = bank(f"r{2 + h}", f"a_ps{h}")
             slots = slice(h * HALF, (h + 1) * HALF)
@@ -139,19 +145,15 @@ def tile_attend_bpagequotas_v_kernel(tc, query, query2, keys_words, keys_scales,
                 out=pa[:, 4 * h : 4 * (h + 1)], in_=a_ps[:].rearrange("p t (g j) -> p j g t", j=4), func=ACT.Exp
             )
 
-        q2_grouped = sb.tile([P, PACK, P, PACK], BF16, name="q2_grouped", align_bytes=64)
-        q2_codes = sb.tile([P, Q], U32, name="q2_codes", align_bytes=64)
-        q2_scales = sb.tile([P, Q], U8, name="q2_scales", align_bytes=64)
-        interleave_query(q2_raw[1], q2_grouped, 1, 0)
-        interleave_query(q2_raw[0], q2_grouped, 0, 64)
         quantize_query(q2_grouped, q2_codes, q2_scales, 0, P)
-        b_ps = bank("g1", "b_ps")
+        msum = sb.tile([P, PACK, G], F32, name="msum")
+        b_ps = [ps.tile([P, 2, P], F32, name=f"b_ps{n}", tag=f"g{n}") for n in range(2)]
         for t in range(PACK):
             cols = slice(t * P, (t + 1) * P)
             for u in range(2):
                 slots = slice(u * HALF, (u + 1) * HALF)
                 nc.tensor.matmul_mx(
-                    out=b_ps[:, t, :],
+                    out=b_ps[t // 2][:, t % 2, :],
                     lhsT=q2_codes[:, cols].bitcast(FP8X4),
                     lhsT_scale=q2_scales[:, cols],
                     rhs=kb[:, slots].bitcast(FP4X4),
@@ -159,14 +161,27 @@ def tile_attend_bpagequotas_v_kernel(tc, query, query2, keys_words, keys_scales,
                     start=(u == 0),
                     stop=(u == 1),
                 )
-        msum = sb.tile([P, PACK, G], F32, name="msum")
-        nc.vector.tensor_reduce(out=msum[:], in_=b_ps[:].rearrange("p t (g j) -> p t g j", j=4), axis=AX.X, op=ALU.add)
+        for n in range(2):
+            nc.vector.tensor_reduce(
+                out=msum[:, 2 * n : 2 * n + 2], in_=b_ps[n][:].rearrange("p t (g j) -> p t g j", j=4), axis=AX.X, op=ALU.add
+            )
         mabs = sb.tile([P, PACK, G], F32, name="mabs")
         nc.scalar.activation(out=mabs[:], in_=msum[:], func=ACT.Abs, scale=3.0 / PAGE)
-        mexp = sb.tile([P, PACK, G], F32, name="mexp")
+        mexp = sb.tile([P, PACK, G], F32, name="mexp", tag="mexp", align_bytes=64)
         nc.scalar.activation(out=mexp[:], in_=mabs[:], func=ACT.Exp, scale=-1.0)
         soft = sb.tile([P, PACK, ROW], F32, name="soft")
         nc.scalar.activation(out=soft[:, :, 0:G], in_=mexp[:], func=ACT.Ln, bias=1.0)
+
+        sum_ps = bank("g0", "sum_ps")
+        for j in range(PAGE):
+            nc.tensor.matmul(
+                sum_ps[:, 0, :], pa[:, j].rearrange("p g t -> p (g t)"), ident[:], is_transpose=True, start=(j == 0), stop=(j == PAGE - 1)
+            )
+        inv_turned = sb.tile([P, P], F32, name="inv_turned")
+        for n in range(4):
+            nc.vector.reciprocal(out=inv_turned[:, 32 * n : 32 * (n + 1)], in_=sum_ps[:, 0, 32 * n : 32 * (n + 1)])
+        inv_ps = bank("g1", "inv_ps")
+        nc.tensor.transpose(inv_ps[:, 0, :], inv_turned[:], ident[:])
 
         relu = sb.tile([P, PACK, ROW], F32, name="relu")
         nc.vector.tensor_copy(out=relu[:, :, G], in_=reserve_sb[:])
@@ -181,32 +196,17 @@ def tile_attend_bpagequotas_v_kernel(tc, query, query2, keys_words, keys_scales,
         inv_z = sb.tile([P, PACK], F32, name="inv_z")
         nc.vector.reciprocal(out=inv_z[:], in_=z[:])
 
-        sum_ps = bank("f0", "sum_ps")
-        for j in range(PAGE):
-            nc.tensor.matmul(
-                sum_ps[:, 0, :], pa[:, j].rearrange("p g t -> p (g t)"), ident[:], is_transpose=True, start=(j == 0), stop=(j == PAGE - 1)
-            )
-        inv_turned = sb.tile([P, P], F32, name="inv_turned")
-        for n in range(4):
-            nc.vector.reciprocal(out=inv_turned[:, 32 * n : 32 * (n + 1)], in_=sum_ps[:, 0, 32 * n : 32 * (n + 1)])
-        inv_ps = bank("f1", "inv_ps")
-        nc.tensor.transpose(inv_ps[:, 0, :], inv_turned[:], ident[:])
-        share = sb.tile([P, G, PACK], F32, name="share")
-        nc.vector.tensor_tensor(
-            out=share[:],
-            in0=inv_ps[:, 0, :].rearrange("p (g t) -> p g t", t=PACK),
-            in1=qs_sb[:].unsqueeze(1).broadcast_to([P, G, PACK]),
-            op=ALU.mult,
-        )
         unnormed = sb.tile([P, G, PACK], F32, name="unnormed")
-        nc.vector.tensor_tensor(out=unnormed[:], in0=quota[:], in1=share[:], op=ALU.mult)
+        nc.vector.tensor_tensor(out=unnormed[:], in0=inv_ps[:, 0, :].rearrange("p (g t) -> p g t", t=PACK), in1=quota[:], op=ALU.mult)
+        row_scale = sb.tile([P, PACK], F32, name="row_scale")
+        nc.vector.tensor_tensor(out=row_scale[:], in0=inv_z[:], in1=qs_sb[:], op=ALU.mult)
         factor = sb.tile([P, G, PACK], F32, name="factor")
-        nc.vector.tensor_tensor(out=factor[:], in0=unnormed[:], in1=inv_z[:].unsqueeze(1).broadcast_to([P, G, PACK]), op=ALU.mult)
+        nc.vector.tensor_tensor(out=factor[:], in0=unnormed[:], in1=row_scale[:].unsqueeze(1).broadcast_to([P, G, PACK]), op=ALU.mult)
 
         w_codes = sb.tile([P, I], U32, name="w_codes", align_bytes=64)
         w_scales = sb.tile([P, I], U8, name="w_scales", align_bytes=64)
         for h in range(2):
-            wq = sb.tile([P, HALF, PACK], BF16, name=f"wq{h}", align_bytes=64)
+            wq = sb.tile([P, HALF, PACK], BF16, name=f"wq{h}", tag=f"wq{h}", align_bytes=64)
             nc.vector.tensor_tensor(
                 out=wq[:].rearrange("p (g j) t -> p g j t", j=PAGE),
                 in0=pa[:, :, h * GH : (h + 1) * GH, :].rearrange("p j g t -> p g j t"),
@@ -216,25 +216,56 @@ def tile_attend_bpagequotas_v_kernel(tc, query, query2, keys_words, keys_scales,
             slots = slice(h * HALF, (h + 1) * HALF)
             nc.vector.quantize_mx(out=w_codes[:, slots].bitcast(FP8X4), scales=w_scales[:, slots], in_=wq[:].rearrange("p i t -> p (i t)"))
 
-        grows_grouped = sb.tile([P, E, PACK], BF16, name="grows_grouped", align_bytes=64)
-        src = grows_raw[:].rearrange("p j (c i) -> p c j i", i=4)
-        dst = grows_grouped[:].rearrange("p (c i) j -> p c j i", i=4)
         g_codes = sb.tile([P, E], U32, name="g_codes", align_bytes=64)
         g_scales = sb.tile([P, E], U8, name="g_scales", align_bytes=64)
-        for k in range(E // P):
-            if k < 3:
-                nc.vector.tensor_copy(out=dst[:, 32 * k : 32 * (k + 1)], in_=src[:, 32 * k : 32 * (k + 1)])
-            else:
-                nc.scalar.copy(out=dst[:, 32 * k : 32 * (k + 1)], in_=src[:, 32 * k : 32 * (k + 1)])
-            cols = slice(k * P, (k + 1) * P)
-            nc.vector.quantize_mx(
-                out=g_codes[:, cols].bitcast(FP8X4), scales=g_scales[:, cols], in_=grows_grouped[:, cols, :].rearrange("p e j -> p (e j)")
-            )
+        src = grows_raw[:].rearrange("p j (c i) -> p c j i", i=4)
+        for n in range(2):
+            grouped = sb.tile([P, E // 2, PACK], BF16, name=f"grows_grouped{n}", tag=("grows_grouped", "wide")[n], align_bytes=64)
+            dst = grouped[:].rearrange("p (c i) j -> p c j i", i=4)
+            for m in range(2):
+                k = 2 * n + m
+                nc.vector.tensor_copy(out=dst[:, 32 * m : 32 * (m + 1)], in_=src[:, 32 * k : 32 * (k + 1)])
+                cols = slice(k * P, (k + 1) * P)
+                nc.vector.quantize_mx(
+                    out=g_codes[:, cols].bitcast(FP8X4),
+                    scales=g_scales[:, cols],
+                    in_=grouped[:, m * P : (m + 1) * P, :].rearrange("p e j -> p (e j)"),
+                )
+
+        fade_ps = bank("r0", "fade_ps")
+        nc.tensor.transpose(fade_ps[:, 0, :], fade_rows[:], ident[:])
+        fade_cols = sb.tile([P, T // P], F32, name="fade_cols")
+        nc.scalar.copy(out=fade_cols[:], in_=fade_ps[:, 0, 0 : T // P])
+
+        turned = [[None, None] for k in range(E // P)]
+
+        def turn_and_fade(k, u):
+            half = sb.tile([P, 4, P], F32, name=f"turned{k}_{u}", tag=TURNED.get((k, u), f"turned{k}_{u}"), align_bytes=64)
+            fwd = bank(FWD[k][u], f"fwd{k}_{u}")
+            for c in range(4):
+                blk = 4 * u + c
+                nc.tensor.transpose(fwd[:, c, :], old_sb[k][:, blk * P : (blk + 1) * P], ident[:])
+            for c in range(4):
+                blk = 4 * u + c
+                nc.scalar.activation(out=half[:, c, :], in_=fwd[:, c, :], func=ACT.Copy, scale=fade_cols[:, blk : blk + 1])
+            turned[k][u] = half
+
+        def turn_back(k, u):
+            bk = bank(BACK[k][u], f"back{k}_{u}")
+            for c in range(4):
+                nc.tensor.transpose(bk[:, c, :], turned[k][u][:, c, :], ident[:])
+            return bk
+
+        back = [[None, None] for k in range(E // P)]
+        turn_and_fade(0, 0)
+        turn_and_fade(0, 1)
+        turn_and_fade(1, 0)
+        back[0] = [turn_back(0, u) for u in range(2)]
 
         pieces = [(0, 0, HALF), (0, HALF, I)] + [(k, 0, I) for k in range(1, E // P)]
         gv = [sb.tile([P, I], F32, name=f"gv{k}") for k in range(E // P)]
         for n, (k, lo, hi) in enumerate(pieces):
-            gv_ps = ps.tile([P, BANK], F32, name=f"gv_ps{n}", tag=f"g{(n + 1) % 2}")
+            gv_ps = ps.tile([P, BANK], F32, name=f"gv_ps{n}", tag=["g0","g1","r2","r3","f1"][n])
             cols = slice(k * P, (k + 1) * P)
             nc.tensor.matmul_mx(
                 out=gv_ps[:, 0 : hi - lo],
@@ -247,78 +278,21 @@ def tile_attend_bpagequotas_v_kernel(tc, query, query2, keys_words, keys_scales,
             )
             nc.scalar.copy(out=gv[k][:, lo:hi], in_=gv_ps[:, 0 : hi - lo])
 
-        fade_ps = bank("r0", "fade_ps")
-        nc.tensor.transpose(fade_ps[:, 0, :], fade_rows[:], ident[:])
-        fade_cols = sb.tile([P, T // P], F32, name="fade_cols")
-        nc.scalar.copy(out=fade_cols[:], in_=fade_ps[:, 0, 0 : T // P])
-
-        fade_wide = None
-
-        def turn_and_fade(k):
-            turned = sb.tile([P, T // P, P], F32, name=f"turned{k}")
-            for u in range(2):
-                fwd = bank(f"f{u}", f"fwd{k}_{u}")
-                for c in range(4):
-                    blk = 4 * u + c
-                    nc.tensor.transpose(fwd[:, c, :], old_sb[k][:, blk * P : (blk + 1) * P], ident[:])
-                for c in range(4):
-                    blk = 4 * u + c
-                    nc.scalar.activation(out=turned[:, blk, :], in_=fwd[:, c, :], func=ACT.Copy, scale=fade_cols[:, blk : blk + 1])
-            return turned
-
-        def turn_back(k, turned):
-            back = []
-            for u in range(2):
-                bk = bank(BACK[k][u], f"back{k}_{u}")
-                for c in range(4):
-                    nc.tensor.transpose(bk[:, c, :], turned[:, 4 * u + c, :], ident[:])
-                back.append(bk)
-            return back
-
-        def store(k, u, res):
-            nc.sync.dma_start(out=out[k * P : (k + 1) * P, u * BANK : (u + 1) * BANK], in_=res)
-
+        turn_and_fade(1, 1)
         for k in range(E // P):
-            route = ROUTE[k]
+            if k > 0:
+                back[k] = [turn_back(k, u) for u in range(2)]
+            if 1 <= k < E // P - 1:
+                turn_and_fade(k + 1, 0)
+                turn_and_fade(k + 1, 1)
             window = placed[k % len(placed)]
-            if route == "GG":
-                faded = sb.tile([P, T], F32, name=f"faded{k}", tag="wide")
-                nc.gpsimd.tensor_tensor(out=faded[:], in0=old_sb[k][:], in1=fade_wide[:], op=ALU.mult)
-            else:
-                turned = turn_and_fade(k)
-            if route in ("V", "G"):
-                back = turn_back(k, turned)
-            if route == "G":
-                faded = sb.tile([P, T], F32, name=f"faded{k}")
-                for u in range(2):
-                    nc.scalar.copy(out=faded[:, u * BANK : (u + 1) * BANK], in_=back[u][:].rearrange("p c n -> p (c n)"))
             for kk, lo, hi in pieces:
                 if kk == k:
                     nc.vector.tensor_copy(window[:].indirect(offsets[:, lo // 16 : hi // 16]), gv[k][:, lo:hi])
-            if route in ("G", "GG"):
-                res = sb.tile([P, T], F32, name=f"res{k}")
-                nc.gpsimd.tensor_tensor(out=res[:], in0=faded[:], in1=window[:], op=ALU.add)
-                nc.sync.dma_start(out=out[k * P : (k + 1) * P, :], in_=res[:])
-            if route == "V":
-                for u in range(2):
-                    res = sb.tile([P, BANK], F32, name=f"res{k}_{u}")
-                    cols = slice(u * BANK, (u + 1) * BANK)
-                    nc.vector.tensor_tensor(out=res[:], in0=back[u][:].rearrange("p c n -> p (c n)"), in1=window[:, cols], op=ALU.add)
-                    store(k, u, res[:])
-            if route == "S":
-                placed_turned = sb.tile([P, T // P, P], F32, name=f"placed_turned{k}", tag="placed_turned")
-                for u in range(2):
-                    fwd = bank(f"f{u}", f"pfwd{k}_{u}")
-                    for c in range(4):
-                        blk = 4 * u + c
-                        nc.tensor.transpose(fwd[:, c, :], window[:, blk * P : (blk + 1) * P], ident[:])
-                    nc.scalar.copy(out=placed_turned[:, 4 * u : 4 * u + 4, :], in_=fwd[:])
-                for u in range(2):
-                    bk = bank(f"r{2 * (k % 2) + u}", f"sum{k}_{u}")
-                    for c in range(4):
-                        blk = 4 * u + c
-                        nc.tensor.matmul(bk[:, c, :], turned[:, blk, :], ident[:], is_transpose=True, start=True, stop=False)
-                        nc.tensor.matmul(bk[:, c, :], placed_turned[:, blk, :], ident[:], is_transpose=True, start=False, stop=True)
-                    res = sb.tile([P, BANK], F32, name=f"res{k}_{u}")
-                    nc.scalar.copy(out=res[:], in_=bk[:].rearrange("p c n -> p (c n)"))
-                    store(k, u, res[:])
+            for lo, hi in ([(0, 512), (512, 768), (768, 1024)] if k == 3 else [(0, 512), (512, 1024)]):
+                res = sb.tile([P, hi - lo], F32, name=f"res{k}_{lo}")
+                u = lo // BANK
+                nc.vector.tensor_tensor(
+                    out=res[:], in0=back[k][u][:].rearrange("p c n -> p (c n)")[:, lo - u * BANK : hi - u * BANK], in1=window[:, lo:hi], op=ALU.add
+                )
+                nc.sync.dma_start(out=out[k * P : (k + 1) * P, lo:hi], in_=res[:])

@@ -23,12 +23,26 @@ PACK = 4
 PAGE = 8
 G = I // PAGE
 HALF = I // 2
-GH = G // 2
 BANK = 512
+BLOCKS = E // P
+TURNS = BANK // P
+PER_COLUMN = 16
 ROW = 40
-BACK = [["r0","r1"],["r3","g0"],["f0","f1"],["r0","r1"]]
-FWD = [["f0","f1"],["f0","g0"],["g1","r2"],["g1","r2"]]
-TURNED = {(0, 0): "mexp"}
+ALIGN = 64
+
+SCALAR_QUERY = 44
+SCALAR_QUERY2 = (40, 20)
+RECIPROCAL_PARTS = 4
+LAST_PART = 256
+
+BANKS_SECOND_SCORES = (0, 1)
+BANK_PAGE_SUMS, BANK_INVERSE_SUMS = 0, 1
+BANKS_FIRST_SCORES = (6, 7)
+BANK_FADE = 4
+BANKS_GV = (0, 1, 2, 3, 6, 7)
+BANKS_TURNED = ((2, 3), (0, 1), (2, 3), (0, 1))
+BANKS_FADED = ((4, 5), (6, 7), (2, 3), (4, 5))
+WINDOW_OF_BLOCK = (0, 1, 2, 1)
 
 
 def tile_attend_bpagequotas_v_kernel(tc, query, query2, keys_words, keys_scales, reserve, qs, grows, old, fade, offs, out):
@@ -37,240 +51,238 @@ def tile_attend_bpagequotas_v_kernel(tc, query, query2, keys_words, keys_scales,
         sb = ctx.enter_context(tc.tile_pool(name="sb", bufs=1))
         ps = ctx.enter_context(tc.psum_pool(name="ps", bufs=1))
 
-        def bank(tag, name):
-            return ps.tile([P, PACK, P], F32, name=name, tag=tag)
+        def psum_tile(bank, name, shape=(P, TURNS, P)):
+            return ps.tile(list(shape), F32, name=name, tag=f"bank{bank}")
 
-        offsets = sb.tile([P, I // 16], U16, name="offsets")
+        offsets = sb.tile([P, I // PER_COLUMN], U16, name="offsets")
         nc.sync.dma_start(offsets[:], offs)
-        key_words = sb.tile([P, T], U16, name="key_words", align_bytes=64)
+        key_words = sb.tile([P, T], U16, name="key_words", align_bytes=ALIGN)
         nc.sync.dma_start(out=key_words[:].bitcast(I32), in_=keys_words[0].bitcast(I32))
-        key_scales = sb.tile([P, T], U8, name="key_scales", align_bytes=64)
+        key_scales = sb.tile([P, T], U8, name="key_scales", align_bytes=ALIGN)
         nc.vector.memset(key_scales[:].bitcast(I32), 0)
-        for quad in range(4):
+        for quadrant in range(4):
             nc.sync.dma_start(
-                out=key_scales[32 * quad : 32 * quad + 4, :].bitcast(I32),
-                in_=keys_scales[0, 4 * quad : 4 * quad + 4, :].bitcast(I32),
+                out=key_scales[32 * quadrant : 32 * quadrant + 4, :].bitcast(I32),
+                in_=keys_scales[0, 4 * quadrant : 4 * quadrant + 4, :].bitcast(I32),
             )
         fade_rows = sb.tile([P, P], F32, name="fade_rows")
         nc.vector.memset(fade_rows[:], 0.0)
         nc.sync.dma_start(out=fade_rows[0 : T // P, :], in_=fade.rearrange("o (c n) -> (o c) n", n=P))
 
-        def load_query(src, name):
-            rows = src.rearrange("(p j) q -> p j q", j=PACK)
-            parts = []
-            for h in range(2):
-                raw = sb.tile([P, PACK, Q // 2], F32, name=f"{name}_raw{h}", tag=("wide" if (name, h) == ("q2", 1) else f"{name}_raw{h}"), align_bytes=64)
-                nc.sync.dma_start(out=raw[:], in_=rows[:, :, h * (Q // 2) : (h + 1) * (Q // 2)])
-                parts.append(raw)
-            return parts
-
-        q1_raw = load_query(query, "q1")
+        q1_raw = sb.tile([P, PACK, Q], F32, name="q1_raw")
+        nc.sync.dma_start(out=q1_raw[:], in_=query.rearrange("(p j) q -> p j q", j=PACK))
         reserve_sb = sb.tile([P, PACK], F32, name="reserve_sb")
         nc.sync.dma_start(out=reserve_sb[:], in_=reserve.rearrange("(p t) o -> p (t o)", t=PACK))
-        q2_raw = load_query(query2, "q2")
+        q2_raw = []
+        for h in range(2):
+            raw = sb.tile([P, PACK, Q // 2], F32, name=f"q2_raw{h}", tag=f"q2_raw{h}", align_bytes=ALIGN)
+            nc.sync.dma_start(out=raw[:], in_=query2.rearrange("(p j) q -> p j q", j=PACK)[:, :, h * Q // 2 : (h + 1) * Q // 2])
+            q2_raw.append(raw)
         grows_raw = sb.tile([P, PACK, E], F32, name="grows_raw")
         nc.sync.dma_start(out=grows_raw[:], in_=grows.rearrange("(p j) e -> p j e", j=PACK))
         qs_sb = sb.tile([P, PACK], F32, name="qs_sb")
         nc.sync.dma_start(out=qs_sb[:], in_=qs.rearrange("(p t) o -> p (t o)", t=PACK))
         old_sb = []
-        for k in range(E // P):
+        for k in range(BLOCKS):
             old_k = sb.tile([P, T], F32, name=f"old{k}")
             nc.sync.dma_start(out=old_k[:], in_=old[k * P : (k + 1) * P, :])
             old_sb.append(old_k)
 
-        ident = sb.tile([P, P], F32, name="ident")
-        make_identity(nc, ident[:])
-        placed = []
-        for k in range(3):
-            placed_k = sb.tile([P, T], F32, name=f"placed{k}")
-            (nc.vector if k < 3 else nc.gpsimd).memset(placed_k[:], 0.0)
-            placed.append(placed_k)
+        identity = sb.tile([P, P], F32, name="identity")
+        make_identity(nc, identity[:])
+        windows = []
+        for n in range(max(WINDOW_OF_BLOCK) + 1):
+            window = sb.tile([P, T], F32, name=f"window{n}")
+            nc.vector.memset(window[:], 0.0)
+            windows.append(window)
 
-        kg = sb.tile([P, I], U16, name="kg", align_bytes=64)
-        nc.vector.tensor_copy(kg[:], key_words[:].indirect(offsets[:]))
-        sg = sb.tile([P, I], U8, name="sg", align_bytes=64)
-        nc.vector.tensor_copy(sg[:], key_scales[:].indirect(offsets[:]))
+        listed_words = sb.tile([P, I], U16, name="listed_words", align_bytes=ALIGN)
+        nc.vector.tensor_copy(listed_words[:], key_words[:].indirect(offsets[:]))
+        listed_scales = sb.tile([P, I], U8, name="listed_scales", align_bytes=ALIGN)
+        nc.vector.tensor_copy(listed_scales[:], key_scales[:].indirect(offsets[:]))
 
-        kb = sb.tile([P, I], U16, name="kb", align_bytes=64)
-        nc.vector.tensor_copy(
-            out=kb[:].rearrange("p (u g j) -> p g u j", u=2, j=4), in_=kg[:].rearrange("p (g u j) -> p g u j", u=2, j=4)
-        )
-        sbb = sb.tile([P, I], U8, name="sbb", align_bytes=64)
-        nc.vector.tensor_copy(
-            out=sbb[:].rearrange("p (u g j) -> p g u j", u=2, j=4), in_=sg[:].rearrange("p (g u j) -> p g u j", u=2, j=4)
-        )
+        def deal(listed, dtype, name):
+            dealt = sb.tile([P, I], dtype, name=name, align_bytes=ALIGN)
+            nc.vector.tensor_copy(
+                out=dealt[:].rearrange("p (u g j) -> p g u j", u=2, j=PAGE // 2),
+                in_=listed[:].rearrange("p (g u j) -> p g u j", u=2, j=PAGE // 2),
+            )
+            return dealt
 
-        def interleave_query(raw, grouped, h, n):
-            src = raw[:].rearrange("p j (s t) -> p s j t", t=PACK)
-            dst = grouped[:, :, 64 * h : 64 * (h + 1), :].rearrange("p t s j -> p s j t")
-            if n > 0:
-                nc.scalar.copy(out=dst[:, 0:n], in_=src[:, 0:n])
-            if n < 64:
-                nc.vector.tensor_copy(out=dst[:, n:64], in_=src[:, n:64])
+        dealt_words = deal(listed_words, U16, "dealt_words")
+        dealt_scales = deal(listed_scales, U8, "dealt_scales")
 
-        def quantize_query(grouped, codes, scales, lo, hi):
-            for t in range(PACK):
-                cols = slice(t * P + lo, t * P + hi)
-                nc.vector.quantize_mx(
-                    out=codes[:, cols].bitcast(FP8X4), scales=scales[:, cols], in_=grouped[:, t, lo:hi, :].rearrange("p s j -> p (s j)")
-                )
+        def cast_query(raw, grouped, scalar_share):
+            src = raw.rearrange("p j (s t) -> p s j t", t=PACK)
+            dst = grouped.rearrange("p t s j -> p s j t")
+            nc.scalar.copy(out=dst[:, :scalar_share], in_=src[:, :scalar_share])
+            nc.vector.tensor_copy(out=dst[:, scalar_share:], in_=src[:, scalar_share:])
 
-        q1_grouped = sb.tile([P, PACK, P, PACK], BF16, name="q1_grouped", align_bytes=64)
-        q1_codes = sb.tile([P, Q], U32, name="q1_codes", align_bytes=64)
-        q1_scales = sb.tile([P, Q], U8, name="q1_scales", align_bytes=64)
-        interleave_query(q1_raw[0], q1_grouped, 0, 48)
-        interleave_query(q1_raw[1], q1_grouped, 1, 20)
-        quantize_query(q1_grouped, q1_codes, q1_scales, 0, P)
-        q2_grouped = sb.tile([P, PACK, P, PACK], BF16, name="q2_grouped", align_bytes=64)
-        q2_codes = sb.tile([P, Q], U32, name="q2_codes", align_bytes=64)
-        q2_scales = sb.tile([P, Q], U8, name="q2_scales", align_bytes=64)
-        interleave_query(q2_raw[1], q2_grouped, 1, 20)
-        interleave_query(q2_raw[0], q2_grouped, 0, 40)
-        pa = sb.tile([P, PAGE, G, PACK], F32, name="pa", tag="wide", align_bytes=64)
-        for h in range(2):
-            a_ps = bank(f"r{2 + h}", f"a_ps{h}")
-            slots = slice(h * HALF, (h + 1) * HALF)
+        def quantize_query(grouped, codes, scales):
             for t in range(PACK):
                 cols = slice(t * P, (t + 1) * P)
-                nc.tensor.matmul_mx(
-                    out=a_ps[:, t, :],
-                    lhsT=q1_codes[:, cols].bitcast(FP8X4),
-                    lhsT_scale=q1_scales[:, cols],
-                    rhs=kb[:, slots].bitcast(FP4X4),
-                    rhs_scale=sbb[:, slots],
-                    start=True,
-                    stop=True,
+                nc.vector.quantize_mx(
+                    out=codes[:, cols].bitcast(FP8X4), scales=scales[:, cols], in_=grouped[:, t].rearrange("p s j -> p (s j)")
                 )
-            nc.scalar.activation(
-                out=pa[:, 4 * h : 4 * (h + 1)], in_=a_ps[:].rearrange("p t (g j) -> p j g t", j=4), func=ACT.Exp
+
+        def score(acc, codes, scales, t, u, start, stop):
+            cols = slice(t * P, (t + 1) * P)
+            slots = slice(u * HALF, (u + 1) * HALF)
+            nc.tensor.matmul_mx(
+                out=acc,
+                lhsT=codes[:, cols].bitcast(FP8X4),
+                lhsT_scale=scales[:, cols],
+                rhs=dealt_words[:, slots].bitcast(FP4X4),
+                rhs_scale=dealt_scales[:, slots],
+                start=start,
+                stop=stop,
             )
 
-        quantize_query(q2_grouped, q2_codes, q2_scales, 0, P)
-        msum = sb.tile([P, PACK, G], F32, name="msum")
-        b_ps = [ps.tile([P, 2, P], F32, name=f"b_ps{n}", tag=f"g{n}") for n in range(2)]
+        q1_grouped = sb.tile([P, PACK, P, PACK], BF16, name="q1_grouped", align_bytes=ALIGN)
+        q1_codes = sb.tile([P, Q], U32, name="q1_codes", align_bytes=ALIGN)
+        q1_scales = sb.tile([P, Q], U8, name="q1_scales", align_bytes=ALIGN)
+        cast_query(q1_raw[:], q1_grouped[:], SCALAR_QUERY)
+        quantize_query(q1_grouped, q1_codes, q1_scales)
+        q2_grouped = sb.tile([P, PACK, P, PACK], BF16, name="q2_grouped", align_bytes=ALIGN)
+        q2_codes = sb.tile([P, Q], U32, name="q2_codes", align_bytes=ALIGN)
+        q2_scales = sb.tile([P, Q], U8, name="q2_scales", align_bytes=ALIGN)
+        for h in (1, 0):
+            cast_query(q2_raw[h][:], q2_grouped[:, :, h * P // 2 : (h + 1) * P // 2, :], SCALAR_QUERY2[h])
+        pa = sb.tile([P, PAGE, G, PACK], F32, name="pa", tag="q2_raw1", align_bytes=ALIGN)
+        for u in range(2):
+            a_ps = psum_tile(BANKS_FIRST_SCORES[u], f"a_ps{u}")
+            for t in range(PACK):
+                score(a_ps[:, t, :], q1_codes, q1_scales, t, u, True, True)
+            nc.scalar.activation(
+                out=pa[:, u * PAGE // 2 : (u + 1) * PAGE // 2], in_=a_ps[:].rearrange("p t (g j) -> p j g t", j=PAGE // 2), func=ACT.Exp
+            )
+
+        quantize_query(q2_grouped, q2_codes, q2_scales)
+        b_sum = sb.tile([P, PACK, G], F32, name="b_sum")
+        b_ps = [psum_tile(bank, f"b_ps{n}", (P, 2, P)) for n, bank in enumerate(BANKS_SECOND_SCORES)]
         for t in range(PACK):
-            cols = slice(t * P, (t + 1) * P)
             for u in range(2):
-                slots = slice(u * HALF, (u + 1) * HALF)
-                nc.tensor.matmul_mx(
-                    out=b_ps[t // 2][:, t % 2, :],
-                    lhsT=q2_codes[:, cols].bitcast(FP8X4),
-                    lhsT_scale=q2_scales[:, cols],
-                    rhs=kb[:, slots].bitcast(FP4X4),
-                    rhs_scale=sbb[:, slots],
-                    start=(u == 0),
-                    stop=(u == 1),
-                )
+                score(b_ps[t // 2][:, t % 2, :], q2_codes, q2_scales, t, u, u == 0, u == 1)
         for n in range(2):
             nc.vector.tensor_reduce(
-                out=msum[:, 2 * n : 2 * n + 2], in_=b_ps[n][:].rearrange("p t (g j) -> p t g j", j=4), axis=AX.X, op=ALU.add
+                out=b_sum[:, 2 * n : 2 * n + 2], in_=b_ps[n][:].rearrange("p t (g j) -> p t g j", j=PAGE // 2), axis=AX.X, op=ALU.add
             )
-        mabs = sb.tile([P, PACK, G], F32, name="mabs")
-        nc.scalar.activation(out=mabs[:], in_=msum[:], func=ACT.Abs, scale=3.0 / PAGE)
-        mexp = sb.tile([P, PACK, G], F32, name="mexp", tag="mexp", align_bytes=64)
-        nc.scalar.activation(out=mexp[:], in_=mabs[:], func=ACT.Exp, scale=-1.0)
-        soft = sb.tile([P, PACK, ROW], F32, name="soft")
-        nc.scalar.activation(out=soft[:, :, 0:G], in_=mexp[:], func=ACT.Ln, bias=1.0)
+        x_abs = sb.tile([P, PACK, G], F32, name="x_abs")
+        nc.scalar.activation(out=x_abs[:], in_=b_sum[:], func=ACT.Abs, scale=3.0 / PAGE)
+        x_exp = sb.tile([P, PACK, G], F32, name="x_exp", tag="after_ln", align_bytes=ALIGN)
+        nc.scalar.activation(out=x_exp[:], in_=x_abs[:], func=ACT.Exp, scale=-1.0)
+        log_part = sb.tile([P, PACK, ROW], F32, name="log_part")
+        nc.scalar.activation(out=log_part[:, :, 0:G], in_=x_exp[:], func=ACT.Ln, bias=1.0)
 
-        sum_ps = bank("g0", "sum_ps")
+        sum_ps = psum_tile(BANK_PAGE_SUMS, "sum_ps")
         for j in range(PAGE):
             nc.tensor.matmul(
-                sum_ps[:, 0, :], pa[:, j].rearrange("p g t -> p (g t)"), ident[:], is_transpose=True, start=(j == 0), stop=(j == PAGE - 1)
+                sum_ps[:, 0, :], pa[:, j].rearrange("p g t -> p (g t)"), identity[:], is_transpose=True, start=(j == 0), stop=(j == PAGE - 1)
             )
-        inv_turned = sb.tile([P, P], F32, name="inv_turned")
-        for n in range(4):
-            nc.vector.reciprocal(out=inv_turned[:, 32 * n : 32 * (n + 1)], in_=sum_ps[:, 0, 32 * n : 32 * (n + 1)])
-        inv_ps = bank("g1", "inv_ps")
-        nc.tensor.transpose(inv_ps[:, 0, :], inv_turned[:], ident[:])
+        inverse_turned = sb.tile([P, P], F32, name="inverse_turned")
+        for n in range(RECIPROCAL_PARTS):
+            cols = slice(n * P // RECIPROCAL_PARTS, (n + 1) * P // RECIPROCAL_PARTS)
+            nc.vector.reciprocal(out=inverse_turned[:, cols], in_=sum_ps[:, 0, cols])
+        inverse_ps = psum_tile(BANK_INVERSE_SUMS, "inverse_ps")
+        nc.tensor.transpose(inverse_ps[:, 0, :], inverse_turned[:], identity[:])
 
-        relu = sb.tile([P, PACK, ROW], F32, name="relu")
-        nc.vector.tensor_copy(out=relu[:, :, G], in_=reserve_sb[:])
-        nc.vector.tensor_scalar(out=relu[:, :, 0:G], in0=msum[:], scalar1=3.0 / PAGE, scalar2=0.0, op0=ALU.mult, op1=ALU.max)
-        nc.vector.tensor_reduce(out=soft[:, :, G], in_=relu[:, :, 0 : G + 1], axis=AX.X, op=ALU.add)
+        positive_part = sb.tile([P, PACK, ROW], F32, name="positive_part")
+        nc.vector.tensor_copy(out=positive_part[:, :, G], in_=reserve_sb[:])
+        nc.vector.tensor_scalar(out=positive_part[:, :, 0:G], in0=b_sum[:], scalar1=3.0 / PAGE, scalar2=0.0, op0=ALU.mult, op1=ALU.max)
+        nc.vector.tensor_reduce(out=log_part[:, :, G], in_=positive_part[:, :, 0 : G + 1], axis=AX.X, op=ALU.add)
         z = sb.tile([P, PACK], F32, name="z")
-        nc.vector.tensor_reduce(out=z[:], in_=soft[:, :, 0 : G + 1], axis=AX.X, op=ALU.add)
-        quota = sb.tile([P, G, PACK], F32, name="quota")
-        nc.vector.tensor_tensor(
-            out=quota[:], in0=soft[:, :, 0:G].rearrange("p t g -> p g t"), in1=relu[:, :, 0:G].rearrange("p t g -> p g t"), op=ALU.add
-        )
-        inv_z = sb.tile([P, PACK], F32, name="inv_z")
-        nc.vector.reciprocal(out=inv_z[:], in_=z[:])
-
-        unnormed = sb.tile([P, G, PACK], F32, name="unnormed")
-        nc.vector.tensor_tensor(out=unnormed[:], in0=inv_ps[:, 0, :].rearrange("p (g t) -> p g t", t=PACK), in1=quota[:], op=ALU.mult)
+        nc.vector.tensor_reduce(out=z[:], in_=log_part[:, :, 0 : G + 1], axis=AX.X, op=ALU.add)
+        quota = sb.tile([P, PACK, G], F32, name="quota")
+        nc.vector.tensor_tensor(out=quota[:], in0=log_part[:, :, 0:G], in1=positive_part[:, :, 0:G], op=ALU.add)
+        inverse_z = sb.tile([P, PACK], F32, name="inverse_z")
+        nc.vector.reciprocal(out=inverse_z[:], in_=z[:])
+        page_share = sb.tile([P, PACK, G], F32, name="page_share")
+        nc.vector.tensor_tensor(out=page_share[:], in0=inverse_ps[:, 0, :].rearrange("p (g t) -> p t g", t=PACK), in1=quota[:], op=ALU.mult)
         row_scale = sb.tile([P, PACK], F32, name="row_scale")
-        nc.vector.tensor_tensor(out=row_scale[:], in0=inv_z[:], in1=qs_sb[:], op=ALU.mult)
+        nc.vector.tensor_tensor(out=row_scale[:], in0=inverse_z[:], in1=qs_sb[:], op=ALU.mult)
         factor = sb.tile([P, G, PACK], F32, name="factor")
-        nc.vector.tensor_tensor(out=factor[:], in0=unnormed[:], in1=row_scale[:].unsqueeze(1).broadcast_to([P, G, PACK]), op=ALU.mult)
+        nc.vector.tensor_tensor(
+            out=factor[:], in0=page_share[:].rearrange("p t g -> p g t"), in1=row_scale[:].unsqueeze(1).broadcast_to([P, G, PACK]), op=ALU.mult
+        )
 
-        w_codes = sb.tile([P, I], U32, name="w_codes", align_bytes=64)
-        w_scales = sb.tile([P, I], U8, name="w_scales", align_bytes=64)
+        w_codes = sb.tile([P, I], U32, name="w_codes", align_bytes=ALIGN)
+        w_scales = sb.tile([P, I], U8, name="w_scales", align_bytes=ALIGN)
         for h in range(2):
-            wq = sb.tile([P, HALF, PACK], BF16, name=f"wq{h}", tag=f"wq{h}", align_bytes=64)
-            nc.vector.tensor_tensor(
-                out=wq[:].rearrange("p (g j) t -> p g j t", j=PAGE),
-                in0=pa[:, :, h * GH : (h + 1) * GH, :].rearrange("p j g t -> p g j t"),
-                in1=factor[:, h * GH : (h + 1) * GH, :].unsqueeze(2).broadcast_to([P, GH, PAGE, PACK]),
-                op=ALU.mult,
-            )
+            wq = sb.tile([P, G // 2, PAGE, PACK], BF16, name=f"wq{h}", tag=f"wq{h}", align_bytes=ALIGN)
+            width = G // 2 // (h + 1)
+            for lo in range(0, G // 2, width):
+                pages = slice(h * G // 2 + lo, h * G // 2 + lo + width)
+                nc.vector.tensor_tensor(
+                    out=wq[:, lo : lo + width],
+                    in0=pa[:, :, pages, :].rearrange("p j g t -> p g j t"),
+                    in1=factor[:, pages, :].unsqueeze(2).broadcast_to([P, width, PAGE, PACK]),
+                    op=ALU.mult,
+                )
             slots = slice(h * HALF, (h + 1) * HALF)
-            nc.vector.quantize_mx(out=w_codes[:, slots].bitcast(FP8X4), scales=w_scales[:, slots], in_=wq[:].rearrange("p i t -> p (i t)"))
+            nc.vector.quantize_mx(
+                out=w_codes[:, slots].bitcast(FP8X4), scales=w_scales[:, slots], in_=wq[:].rearrange("p g j t -> p (g j t)")
+            )
 
-        g_codes = sb.tile([P, E], U32, name="g_codes", align_bytes=64)
-        g_scales = sb.tile([P, E], U8, name="g_scales", align_bytes=64)
-        src = grows_raw[:].rearrange("p j (c i) -> p c j i", i=4)
-        for n in range(2):
-            grouped = sb.tile([P, E // 2, PACK], BF16, name=f"grows_grouped{n}", tag=("grows_grouped", "wide")[n], align_bytes=64)
+        g_codes = []
+        g_scales = sb.tile([P, E], U8, name="g_scales", align_bytes=ALIGN)
+        grows_src = grows_raw[:].rearrange("p j (c i) -> p c j i", i=4)
+
+        def quantize_grows(pair, copy, grouped_tag, codes_tag):
+            codes = sb.tile([P, 2 * P], U32, name=f"g_codes{pair}", tag=codes_tag, align_bytes=ALIGN)
+            g_codes.extend([codes[:, 0:P], codes[:, P : 2 * P]])
+            grouped = sb.tile([P, 2 * P, PACK], BF16, name=f"grows_grouped{pair}", tag=grouped_tag, align_bytes=ALIGN)
             dst = grouped[:].rearrange("p (c i) j -> p c j i", i=4)
             for m in range(2):
-                k = 2 * n + m
-                nc.vector.tensor_copy(out=dst[:, 32 * m : 32 * (m + 1)], in_=src[:, 32 * k : 32 * (k + 1)])
-                cols = slice(k * P, (k + 1) * P)
+                k = 2 * pair + m
+                copy(out=dst[:, m * P // 4 : (m + 1) * P // 4], in_=grows_src[:, k * P // 4 : (k + 1) * P // 4])
                 nc.vector.quantize_mx(
-                    out=g_codes[:, cols].bitcast(FP8X4),
-                    scales=g_scales[:, cols],
+                    out=g_codes[k].bitcast(FP8X4),
+                    scales=g_scales[:, k * P : (k + 1) * P],
                     in_=grouped[:, m * P : (m + 1) * P, :].rearrange("p e j -> p (e j)"),
                 )
 
-        fade_ps = bank("r0", "fade_ps")
-        nc.tensor.transpose(fade_ps[:, 0, :], fade_rows[:], ident[:])
+        quantize_grows(0, nc.vector.tensor_copy, "grows_grouped0", "g_codes0")
+
+        fade_ps = psum_tile(BANK_FADE, "fade_ps")
+        nc.tensor.transpose(fade_ps[:, 0, :], fade_rows[:], identity[:])
         fade_cols = sb.tile([P, T // P], F32, name="fade_cols")
         nc.scalar.copy(out=fade_cols[:], in_=fade_ps[:, 0, 0 : T // P])
 
-        turned = [[None, None] for k in range(E // P)]
+        def turn_and_fade(k):
+            halves = []
+            for u in range(2):
+                tag = "after_ln" if (k, u) == (0, 0) else f"turned{k}_{u}"
+                turned = sb.tile([P, TURNS, P], F32, name=f"turned{k}_{u}", tag=tag, align_bytes=ALIGN)
+                turned_ps = psum_tile(BANKS_TURNED[k][u], f"turned_ps{k}_{u}")
+                for c in range(TURNS):
+                    group = TURNS * u + c
+                    nc.tensor.transpose(turned_ps[:, c, :], old_sb[k][:, group * P : (group + 1) * P], identity[:])
+                for c in range(TURNS):
+                    group = TURNS * u + c
+                    nc.scalar.activation(out=turned[:, c, :], in_=turned_ps[:, c, :], func=ACT.Copy, scale=fade_cols[:, group : group + 1])
+                halves.append(turned)
+            return halves
 
-        def turn_and_fade(k, u):
-            half = sb.tile([P, 4, P], F32, name=f"turned{k}_{u}", tag=TURNED.get((k, u), f"turned{k}_{u}"), align_bytes=64)
-            fwd = bank(FWD[k][u], f"fwd{k}_{u}")
-            for c in range(4):
-                blk = 4 * u + c
-                nc.tensor.transpose(fwd[:, c, :], old_sb[k][:, blk * P : (blk + 1) * P], ident[:])
-            for c in range(4):
-                blk = 4 * u + c
-                nc.scalar.activation(out=half[:, c, :], in_=fwd[:, c, :], func=ACT.Copy, scale=fade_cols[:, blk : blk + 1])
-            turned[k][u] = half
+        def turn_back(k, halves):
+            banks = []
+            for u in range(2):
+                faded_ps = psum_tile(BANKS_FADED[k][u], f"faded_ps{k}_{u}")
+                for c in range(TURNS):
+                    nc.tensor.transpose(faded_ps[:, c, :], halves[u][:, c, :], identity[:])
+                banks.append(faded_ps)
+            return banks
 
-        def turn_back(k, u):
-            bk = bank(BACK[k][u], f"back{k}_{u}")
-            for c in range(4):
-                nc.tensor.transpose(bk[:, c, :], turned[k][u][:, c, :], ident[:])
-            return bk
+        faded = turn_back(0, turn_and_fade(0))
+        quantize_grows(1, nc.scalar.copy, "after_ln", "wq1")
 
-        back = [[None, None] for k in range(E // P)]
-        turn_and_fade(0, 0)
-        turn_and_fade(0, 1)
-        turn_and_fade(1, 0)
-        back[0] = [turn_back(0, u) for u in range(2)]
-
-        pieces = [(0, 0, HALF), (0, HALF, I)] + [(k, 0, I) for k in range(1, E // P)]
-        gv = [sb.tile([P, I], F32, name=f"gv{k}") for k in range(E // P)]
+        pieces = [(k, lo, lo + HALF) for lo in (0, HALF) for k in range(2)] + [(k, 0, I) for k in range(2, BLOCKS)]
+        gv = [sb.tile([P, I], F32, name=f"gv{k}") for k in range(BLOCKS)]
         for n, (k, lo, hi) in enumerate(pieces):
-            gv_ps = ps.tile([P, BANK], F32, name=f"gv_ps{n}", tag=["g0","g1","r2","r3","f1"][n])
-            cols = slice(k * P, (k + 1) * P)
+            gv_ps = psum_tile(BANKS_GV[n], f"gv_ps{n}", (P, BANK))
             nc.tensor.matmul_mx(
                 out=gv_ps[:, 0 : hi - lo],
-                lhsT=g_codes[:, cols].bitcast(FP8X4),
-                lhsT_scale=g_scales[:, cols],
+                lhsT=g_codes[k].bitcast(FP8X4),
+                lhsT_scale=g_scales[:, k * P : (k + 1) * P],
                 rhs=w_codes[:, lo:hi].bitcast(FP8X4),
                 rhs_scale=w_scales[:, lo:hi],
                 start=True,
@@ -278,21 +290,32 @@ def tile_attend_bpagequotas_v_kernel(tc, query, query2, keys_words, keys_scales,
             )
             nc.scalar.copy(out=gv[k][:, lo:hi], in_=gv_ps[:, 0 : hi - lo])
 
-        turn_and_fade(1, 1)
-        for k in range(E // P):
-            if k > 0:
-                back[k] = [turn_back(k, u) for u in range(2)]
-            if 1 <= k < E // P - 1:
-                turn_and_fade(k + 1, 0)
-                turn_and_fade(k + 1, 1)
-            window = placed[k % len(placed)]
-            for kk, lo, hi in pieces:
-                if kk == k:
-                    nc.vector.tensor_copy(window[:].indirect(offsets[:, lo // 16 : hi // 16]), gv[k][:, lo:hi])
-            for lo, hi in ([(0, 512), (512, 768), (768, 1024)] if k == 3 else [(0, 512), (512, 1024)]):
-                res = sb.tile([P, hi - lo], F32, name=f"res{k}_{lo}")
+        def scatter(k, lo, hi):
+            window = windows[WINDOW_OF_BLOCK[k]]
+            nc.vector.tensor_copy(window[:].indirect(offsets[:, lo // PER_COLUMN : hi // PER_COLUMN]), gv[k][:, lo:hi])
+
+        def add_and_store(k, banks):
+            cuts = [0, BANK, T - LAST_PART, T] if k == BLOCKS - 1 else [0, BANK, T]
+            for lo, hi in zip(cuts, cuts[1:]):
                 u = lo // BANK
+                result = sb.tile([P, hi - lo], F32, name=f"result{k}_{lo}")
                 nc.vector.tensor_tensor(
-                    out=res[:], in0=back[k][u][:].rearrange("p c n -> p (c n)")[:, lo - u * BANK : hi - u * BANK], in1=window[:, lo:hi], op=ALU.add
+                    out=result[:],
+                    in0=banks[u][:].rearrange("p c n -> p (c n)")[:, lo - u * BANK : hi - u * BANK],
+                    in1=windows[WINDOW_OF_BLOCK[k]][:, lo:hi],
+                    op=ALU.add,
                 )
-                nc.sync.dma_start(out=out[k * P : (k + 1) * P, lo:hi], in_=res[:])
+                nc.sync.dma_start(out=out[k * P : (k + 1) * P, lo:hi], in_=result[:])
+
+        for k, lo, hi in pieces:
+            if k < 2:
+                scatter(k, lo, hi)
+        halves = turn_and_fade(1)
+        add_and_store(0, faded)
+        for k in range(1, BLOCKS):
+            faded = turn_back(k, halves)
+            if k + 1 < BLOCKS:
+                halves = turn_and_fade(k + 1)
+            if k >= 2:
+                scatter(k, 0, I)
+            add_and_store(k, faded)

from contextlib import ExitStack

import concourse.mybir as mybir
from concourse.masks import make_identity

D, E, T, I, Q = 512, 512, 1024, 256, 512
FLOPS = 2 * (2 * D * Q * I + Q * E * I)

F32 = mybir.dt.float32
BF16 = mybir.dt.bfloat16
I32 = mybir.dt.int32
U32 = mybir.dt.uint32
U16 = mybir.dt.uint16
U8 = mybir.dt.uint8
FP8X4 = mybir.dt.float8_e4m3fn_x4
FP4X4 = mybir.dt.float4_e2m1fn_x4
ALU = mybir.AluOpType
ACT = mybir.ActivationFunctionType
AX = mybir.AxisListType

P = 128
PACK = 4
PAGE = 8
G = I // PAGE
HALF = I // 2
BANK = 512
BLOCKS = E // P
TURNS = BANK // P
PER_COLUMN = 16
ROW = 40
ALIGN = 64

SCALAR_QUERY = 44
SCALAR_QUERY2 = (40, 20)
RECIPROCAL_PARTS = 4
LAST_PART = 256

BANKS_SECOND_SCORES = (0, 1)
BANK_PAGE_SUMS, BANK_INVERSE_SUMS = 0, 1
BANKS_FIRST_SCORES = (6, 7)
BANK_FADE = 4
BANKS_GV = (0, 1, 2, 3, 6, 7)
BANKS_TURNED = ((2, 3), (0, 1), (2, 3), (0, 1))
BANKS_FADED = ((4, 5), (6, 7), (2, 3), (4, 5))
WINDOW_OF_BLOCK = (0, 1, 2, 1)


def tile_attend_bpagequotas_v_kernel(tc, query, query2, keys_words, keys_scales, reserve, qs, grows, old, fade, offs, out):
    nc = tc.nc
    with ExitStack() as ctx:
        sb = ctx.enter_context(tc.tile_pool(name="sb", bufs=1))
        ps = ctx.enter_context(tc.psum_pool(name="ps", bufs=1))

        def psum_tile(bank, name, shape=(P, TURNS, P)):
            return ps.tile(list(shape), F32, name=name, tag=f"bank{bank}")

        offsets = sb.tile([P, I // PER_COLUMN], U16, name="offsets")
        nc.sync.dma_start(offsets[:], offs)
        key_words = sb.tile([P, T], U16, name="key_words", align_bytes=ALIGN)
        nc.sync.dma_start(out=key_words[:].bitcast(I32), in_=keys_words[0].bitcast(I32))
        key_scales = sb.tile([P, T], U8, name="key_scales", align_bytes=ALIGN)
        nc.vector.memset(key_scales[:].bitcast(I32), 0)
        for quadrant in range(4):
            nc.sync.dma_start(
                out=key_scales[32 * quadrant : 32 * quadrant + 4, :].bitcast(I32),
                in_=keys_scales[0, 4 * quadrant : 4 * quadrant + 4, :].bitcast(I32),
            )
        fade_rows = sb.tile([P, P], F32, name="fade_rows")
        nc.vector.memset(fade_rows[:], 0.0)
        nc.sync.dma_start(out=fade_rows[0 : T // P, :], in_=fade.rearrange("o (c n) -> (o c) n", n=P))

        q1_raw = sb.tile([P, PACK, Q], F32, name="q1_raw")
        nc.sync.dma_start(out=q1_raw[:], in_=query.rearrange("(p j) q -> p j q", j=PACK))
        reserve_sb = sb.tile([P, PACK], F32, name="reserve_sb")
        nc.sync.dma_start(out=reserve_sb[:], in_=reserve.rearrange("(p t) o -> p (t o)", t=PACK))
        q2_raw = []
        for h in range(2):
            raw = sb.tile([P, PACK, Q // 2], F32, name=f"q2_raw{h}", tag=f"q2_raw{h}", align_bytes=ALIGN)
            nc.sync.dma_start(out=raw[:], in_=query2.rearrange("(p j) q -> p j q", j=PACK)[:, :, h * Q // 2 : (h + 1) * Q // 2])
            q2_raw.append(raw)
        grows_raw = sb.tile([P, PACK, E], F32, name="grows_raw")
        nc.sync.dma_start(out=grows_raw[:], in_=grows.rearrange("(p j) e -> p j e", j=PACK))
        qs_sb = sb.tile([P, PACK], F32, name="qs_sb")
        nc.sync.dma_start(out=qs_sb[:], in_=qs.rearrange("(p t) o -> p (t o)", t=PACK))
        old_sb = []
        for k in range(BLOCKS):
            old_k = sb.tile([P, T], F32, name=f"old{k}")
            nc.sync.dma_start(out=old_k[:], in_=old[k * P : (k + 1) * P, :])
            old_sb.append(old_k)

        identity = sb.tile([P, P], F32, name="identity")
        make_identity(nc, identity[:])
        windows = []
        for n in range(max(WINDOW_OF_BLOCK) + 1):
            window = sb.tile([P, T], F32, name=f"window{n}")
            nc.vector.memset(window[:], 0.0)
            windows.append(window)

        listed_words = sb.tile([P, I], U16, name="listed_words", align_bytes=ALIGN)
        nc.vector.tensor_copy(listed_words[:], key_words[:].indirect(offsets[:]))
        listed_scales = sb.tile([P, I], U8, name="listed_scales", align_bytes=ALIGN)
        nc.vector.tensor_copy(listed_scales[:], key_scales[:].indirect(offsets[:]))

        def deal(listed, dtype, name):
            dealt = sb.tile([P, I], dtype, name=name, align_bytes=ALIGN)
            nc.vector.tensor_copy(
                out=dealt[:].rearrange("p (u g j) -> p g u j", u=2, j=PAGE // 2),
                in_=listed[:].rearrange("p (g u j) -> p g u j", u=2, j=PAGE // 2),
            )
            return dealt

        dealt_words = deal(listed_words, U16, "dealt_words")
        dealt_scales = deal(listed_scales, U8, "dealt_scales")

        def cast_query(raw, grouped, scalar_share):
            src = raw.rearrange("p j (s t) -> p s j t", t=PACK)
            dst = grouped.rearrange("p t s j -> p s j t")
            nc.scalar.copy(out=dst[:, :scalar_share], in_=src[:, :scalar_share])
            nc.vector.tensor_copy(out=dst[:, scalar_share:], in_=src[:, scalar_share:])

        def quantize_query(grouped, codes, scales):
            for t in range(PACK):
                cols = slice(t * P, (t + 1) * P)
                nc.vector.quantize_mx(
                    out=codes[:, cols].bitcast(FP8X4), scales=scales[:, cols], in_=grouped[:, t].rearrange("p s j -> p (s j)")
                )

        def score(acc, codes, scales, t, u, start, stop):
            cols = slice(t * P, (t + 1) * P)
            slots = slice(u * HALF, (u + 1) * HALF)
            nc.tensor.matmul_mx(
                out=acc,
                lhsT=codes[:, cols].bitcast(FP8X4),
                lhsT_scale=scales[:, cols],
                rhs=dealt_words[:, slots].bitcast(FP4X4),
                rhs_scale=dealt_scales[:, slots],
                start=start,
                stop=stop,
            )

        q1_grouped = sb.tile([P, PACK, P, PACK], BF16, name="q1_grouped", align_bytes=ALIGN)
        q1_codes = sb.tile([P, Q], U32, name="q1_codes", align_bytes=ALIGN)
        q1_scales = sb.tile([P, Q], U8, name="q1_scales", align_bytes=ALIGN)
        cast_query(q1_raw[:], q1_grouped[:], SCALAR_QUERY)
        quantize_query(q1_grouped, q1_codes, q1_scales)
        q2_grouped = sb.tile([P, PACK, P, PACK], BF16, name="q2_grouped", align_bytes=ALIGN)
        q2_codes = sb.tile([P, Q], U32, name="q2_codes", align_bytes=ALIGN)
        q2_scales = sb.tile([P, Q], U8, name="q2_scales", align_bytes=ALIGN)
        for h in (1, 0):
            cast_query(q2_raw[h][:], q2_grouped[:, :, h * P // 2 : (h + 1) * P // 2, :], SCALAR_QUERY2[h])
        pa = sb.tile([P, PAGE, G, PACK], F32, name="pa", tag="q2_raw1", align_bytes=ALIGN)
        for u in range(2):
            a_ps = psum_tile(BANKS_FIRST_SCORES[u], f"a_ps{u}")
            for t in range(PACK):
                score(a_ps[:, t, :], q1_codes, q1_scales, t, u, True, True)
            nc.scalar.activation(
                out=pa[:, u * PAGE // 2 : (u + 1) * PAGE // 2], in_=a_ps[:].rearrange("p t (g j) -> p j g t", j=PAGE // 2), func=ACT.Exp
            )

        quantize_query(q2_grouped, q2_codes, q2_scales)
        b_sum = sb.tile([P, PACK, G], F32, name="b_sum")
        b_ps = [psum_tile(bank, f"b_ps{n}", (P, 2, P)) for n, bank in enumerate(BANKS_SECOND_SCORES)]
        for t in range(PACK):
            for u in range(2):
                score(b_ps[t // 2][:, t % 2, :], q2_codes, q2_scales, t, u, u == 0, u == 1)
        for n in range(2):
            nc.vector.tensor_reduce(
                out=b_sum[:, 2 * n : 2 * n + 2], in_=b_ps[n][:].rearrange("p t (g j) -> p t g j", j=PAGE // 2), axis=AX.X, op=ALU.add
            )
        x_abs = sb.tile([P, PACK, G], F32, name="x_abs")
        nc.scalar.activation(out=x_abs[:], in_=b_sum[:], func=ACT.Abs, scale=3.0 / PAGE)
        x_exp = sb.tile([P, PACK, G], F32, name="x_exp", tag="after_ln", align_bytes=ALIGN)
        nc.scalar.activation(out=x_exp[:], in_=x_abs[:], func=ACT.Exp, scale=-1.0)
        log_part = sb.tile([P, PACK, ROW], F32, name="log_part")
        nc.scalar.activation(out=log_part[:, :, 0:G], in_=x_exp[:], func=ACT.Ln, bias=1.0)

        sum_ps = psum_tile(BANK_PAGE_SUMS, "sum_ps")
        for j in range(PAGE):
            nc.tensor.matmul(
                sum_ps[:, 0, :], pa[:, j].rearrange("p g t -> p (g t)"), identity[:], is_transpose=True, start=(j == 0), stop=(j == PAGE - 1)
            )
        inverse_turned = sb.tile([P, P], F32, name="inverse_turned")
        for n in range(RECIPROCAL_PARTS):
            cols = slice(n * P // RECIPROCAL_PARTS, (n + 1) * P // RECIPROCAL_PARTS)
            nc.vector.reciprocal(out=inverse_turned[:, cols], in_=sum_ps[:, 0, cols])
        inverse_ps = psum_tile(BANK_INVERSE_SUMS, "inverse_ps")
        nc.tensor.transpose(inverse_ps[:, 0, :], inverse_turned[:], identity[:])

        positive_part = sb.tile([P, PACK, ROW], F32, name="positive_part")
        nc.vector.tensor_copy(out=positive_part[:, :, G], in_=reserve_sb[:])
        nc.vector.tensor_scalar(out=positive_part[:, :, 0:G], in0=b_sum[:], scalar1=3.0 / PAGE, scalar2=0.0, op0=ALU.mult, op1=ALU.max)
        nc.vector.tensor_reduce(out=log_part[:, :, G], in_=positive_part[:, :, 0 : G + 1], axis=AX.X, op=ALU.add)
        z = sb.tile([P, PACK], F32, name="z")
        nc.vector.tensor_reduce(out=z[:], in_=log_part[:, :, 0 : G + 1], axis=AX.X, op=ALU.add)
        quota = sb.tile([P, PACK, G], F32, name="quota")
        nc.vector.tensor_tensor(out=quota[:], in0=log_part[:, :, 0:G], in1=positive_part[:, :, 0:G], op=ALU.add)
        inverse_z = sb.tile([P, PACK], F32, name="inverse_z")
        nc.vector.reciprocal(out=inverse_z[:], in_=z[:])
        page_share = sb.tile([P, PACK, G], F32, name="page_share")
        nc.vector.tensor_tensor(out=page_share[:], in0=inverse_ps[:, 0, :].rearrange("p (g t) -> p t g", t=PACK), in1=quota[:], op=ALU.mult)
        row_scale = sb.tile([P, PACK], F32, name="row_scale")
        nc.vector.tensor_tensor(out=row_scale[:], in0=inverse_z[:], in1=qs_sb[:], op=ALU.mult)
        factor = sb.tile([P, G, PACK], F32, name="factor")
        nc.vector.tensor_tensor(
            out=factor[:], in0=page_share[:].rearrange("p t g -> p g t"), in1=row_scale[:].unsqueeze(1).broadcast_to([P, G, PACK]), op=ALU.mult
        )

        w_codes = sb.tile([P, I], U32, name="w_codes", align_bytes=ALIGN)
        w_scales = sb.tile([P, I], U8, name="w_scales", align_bytes=ALIGN)
        for h in range(2):
            wq = sb.tile([P, G // 2, PAGE, PACK], BF16, name=f"wq{h}", tag=f"wq{h}", align_bytes=ALIGN)
            width = G // 2 // (h + 1)
            for lo in range(0, G // 2, width):
                pages = slice(h * G // 2 + lo, h * G // 2 + lo + width)
                nc.vector.tensor_tensor(
                    out=wq[:, lo : lo + width],
                    in0=pa[:, :, pages, :].rearrange("p j g t -> p g j t"),
                    in1=factor[:, pages, :].unsqueeze(2).broadcast_to([P, width, PAGE, PACK]),
                    op=ALU.mult,
                )
            slots = slice(h * HALF, (h + 1) * HALF)
            nc.vector.quantize_mx(
                out=w_codes[:, slots].bitcast(FP8X4), scales=w_scales[:, slots], in_=wq[:].rearrange("p g j t -> p (g j t)")
            )

        g_codes = []
        g_scales = sb.tile([P, E], U8, name="g_scales", align_bytes=ALIGN)
        grows_src = grows_raw[:].rearrange("p j (c i) -> p c j i", i=4)

        def quantize_grows(pair, copy, grouped_tag, codes_tag):
            codes = sb.tile([P, 2 * P], U32, name=f"g_codes{pair}", tag=codes_tag, align_bytes=ALIGN)
            g_codes.extend([codes[:, 0:P], codes[:, P : 2 * P]])
            grouped = sb.tile([P, 2 * P, PACK], BF16, name=f"grows_grouped{pair}", tag=grouped_tag, align_bytes=ALIGN)
            dst = grouped[:].rearrange("p (c i) j -> p c j i", i=4)
            for m in range(2):
                k = 2 * pair + m
                copy(out=dst[:, m * P // 4 : (m + 1) * P // 4], in_=grows_src[:, k * P // 4 : (k + 1) * P // 4])
                nc.vector.quantize_mx(
                    out=g_codes[k].bitcast(FP8X4),
                    scales=g_scales[:, k * P : (k + 1) * P],
                    in_=grouped[:, m * P : (m + 1) * P, :].rearrange("p e j -> p (e j)"),
                )

        quantize_grows(0, nc.vector.tensor_copy, "grows_grouped0", "g_codes0")

        fade_ps = psum_tile(BANK_FADE, "fade_ps")
        nc.tensor.transpose(fade_ps[:, 0, :], fade_rows[:], identity[:])
        fade_cols = sb.tile([P, T // P], F32, name="fade_cols")
        nc.scalar.copy(out=fade_cols[:], in_=fade_ps[:, 0, 0 : T // P])

        def turn_and_fade(k):
            halves = []
            for u in range(2):
                tag = "after_ln" if (k, u) == (0, 0) else f"turned{k}_{u}"
                turned = sb.tile([P, TURNS, P], F32, name=f"turned{k}_{u}", tag=tag, align_bytes=ALIGN)
                turned_ps = psum_tile(BANKS_TURNED[k][u], f"turned_ps{k}_{u}")
                for c in range(TURNS):
                    group = TURNS * u + c
                    nc.tensor.transpose(turned_ps[:, c, :], old_sb[k][:, group * P : (group + 1) * P], identity[:])
                for c in range(TURNS):
                    group = TURNS * u + c
                    nc.scalar.activation(out=turned[:, c, :], in_=turned_ps[:, c, :], func=ACT.Copy, scale=fade_cols[:, group : group + 1])
                halves.append(turned)
            return halves

        def turn_back(k, halves):
            banks = []
            for u in range(2):
                faded_ps = psum_tile(BANKS_FADED[k][u], f"faded_ps{k}_{u}")
                for c in range(TURNS):
                    nc.tensor.transpose(faded_ps[:, c, :], halves[u][:, c, :], identity[:])
                banks.append(faded_ps)
            return banks

        faded = turn_back(0, turn_and_fade(0))
        quantize_grows(1, nc.scalar.copy, "after_ln", "wq1")

        pieces = [(k, lo, lo + HALF) for lo in (0, HALF) for k in range(2)] + [(k, 0, I) for k in range(2, BLOCKS)]
        gv = [sb.tile([P, I], F32, name=f"gv{k}") for k in range(BLOCKS)]
        for n, (k, lo, hi) in enumerate(pieces):
            gv_ps = psum_tile(BANKS_GV[n], f"gv_ps{n}", (P, BANK))
            nc.tensor.matmul_mx(
                out=gv_ps[:, 0 : hi - lo],
                lhsT=g_codes[k].bitcast(FP8X4),
                lhsT_scale=g_scales[:, k * P : (k + 1) * P],
                rhs=w_codes[:, lo:hi].bitcast(FP8X4),
                rhs_scale=w_scales[:, lo:hi],
                start=True,
                stop=True,
            )
            nc.scalar.copy(out=gv[k][:, lo:hi], in_=gv_ps[:, 0 : hi - lo])

        def scatter(k, lo, hi):
            window = windows[WINDOW_OF_BLOCK[k]]
            nc.vector.tensor_copy(window[:].indirect(offsets[:, lo // PER_COLUMN : hi // PER_COLUMN]), gv[k][:, lo:hi])

        def add_and_store(k, banks):
            cuts = [0, BANK, T - LAST_PART, T] if k == BLOCKS - 1 else [0, BANK, T]
            for lo, hi in zip(cuts, cuts[1:]):
                u = lo // BANK
                result = sb.tile([P, hi - lo], F32, name=f"result{k}_{lo}")
                nc.vector.tensor_tensor(
                    out=result[:],
                    in0=banks[u][:].rearrange("p c n -> p (c n)")[:, lo - u * BANK : hi - u * BANK],
                    in1=windows[WINDOW_OF_BLOCK[k]][:, lo:hi],
                    op=ALU.add,
                )
                nc.sync.dma_start(out=out[k * P : (k + 1) * P, lo:hi], in_=result[:])

        for k, lo, hi in pieces:
            if k < 2:
                scatter(k, lo, hi)
        halves = turn_and_fade(1)
        add_and_store(0, faded)
        for k in range(1, BLOCKS):
            faded = turn_back(k, halves)
            if k + 1 < BLOCKS:
                halves = turn_and_fade(k + 1)
            if k >= 2:
                scatter(k, 0, I)
            add_and_store(k, faded)
